import numpy as np
import ml_dtypes


def mxq(x, axis, fmt="e4m3"):
    dtype, down = {"e4m3": (ml_dtypes.float8_e4m3fn, 7), "e5m2": (ml_dtypes.float8_e5m2, 14)}[fmt]
    v = np.moveaxis(np.asarray(x, np.float32).astype(ml_dtypes.bfloat16).astype(np.float64), axis, -1)
    blocks = v.reshape(v.shape[:-1] + (-1, 32))
    amax = np.abs(blocks).max(-1, keepdims=True)
    byte = np.maximum(np.where(amax > 0, np.frexp(amax)[1] - 1 + 127, 0) - down, 1)
    scale = np.exp2(byte - 127.0)
    codes = (blocks / scale).astype(np.float32).astype(dtype).astype(np.float64)
    return np.moveaxis((codes * scale).reshape(v.shape), -1, axis)


WIDE = False


def mx_kscale(k):
    if not WIDE:
        return np.ones(k)
    levels = np.array([24, -24, 12, -12, 0])
    if k % 512:
        return np.exp2(np.random.permutation(np.resize(levels, k // 32))).repeat(32)
    a = np.empty((k // 512, 16))
    for p in range(k // 512):
        a[p, :8] = np.random.permutation(np.resize(levels, 8))
        for g in range(8):
            far = levels[np.abs(levels - a[p, g]) >= 10]
            a[p, g + 8] = far[np.random.randint(len(far))]
    return np.exp2(a.ravel()).repeat(32)


def f64(x):
    return np.asarray(x).astype(np.float64)


def striped8(idx):
    return np.concatenate([v.reshape(-1, 16).T for v in idx]).astype(np.uint16)


def unstriped8(offs):
    return np.stack([offs[16 * g:16 * g + 16].T.reshape(-1) for g in range(8)]).astype(np.int64)


E2M1 = np.array([0.0, 0.5, 1.0, 1.5, 2.0, 3.0, 4.0, 6.0, -0.0, -0.5, -1.0, -1.5, -2.0, -3.0, -4.0, -6.0])


def pack_weight(w, fmt):
    k, n = w.shape
    w = f64(np.asarray(w, np.float32).astype(ml_dtypes.bfloat16)).reshape(k // 32, 32, n)
    amax = np.abs(w).max(1)
    if fmt == "e4m3":
        byte = np.frexp(amax)[1] - 1 + 127 - 7
    else:
        mant, ex = np.frexp(amax / 6.0)
        byte = np.where(mant > 0.5, ex, ex - 1) + 127
    byte = np.clip(np.where(amax > 0, byte, 1), 1, 254)
    scaled = (w * np.exp2(127.0 - byte)[:, None, :]).reshape(k, n).astype(np.float32)
    by_word = np.ascontiguousarray(scaled.reshape(k // 512, 128, 4, n).transpose(0, 1, 3, 2))
    if fmt == "e4m3":
        words = by_word.astype(ml_dtypes.float8_e4m3fn).view(np.uint8)
    else:
        c = by_word.astype(ml_dtypes.float4_e2m1fn).view(np.uint8) & 0xF
        words = (c[..., 0::2] | (c[..., 1::2] << 4)).reshape(k // 512, 128, 2 * n)
    return np.ascontiguousarray(words), np.ascontiguousarray(byte.astype(np.uint8).reshape(k // 512, 16, n))


def unpack_weight(words, scales, fmt):
    g, _, n = scales.shape
    words = np.ascontiguousarray(words).reshape(g, 128, n, -1)
    if fmt == "e4m3":
        vals = words.view(ml_dtypes.float8_e4m3fn).astype(np.float64)
    else:
        nib = np.empty((g, 128, n, 4), np.uint8)
        nib[..., 0::2] = words & 0xF
        nib[..., 1::2] = words >> 4
        vals = E2M1[nib]
    vals = vals * np.repeat(np.exp2(scales.astype(np.float64) - 127.0), 8, axis=1)[..., None]
    return vals.transpose(0, 1, 3, 2).reshape(g * 512, n)


K, R, N, T, J = 1024, 512, 512, 2048, 1024


def setup_inputs():
    n = np.random.standard_normal
    s = mx_kscale(K)[:, None]
    u = mx_kscale(R)[:, None]
    p_wg = pack_weight(n((K, R)) / np.sqrt(K) / s, "e2m1")
    return {
        "xT": (n((K, T)) * s).astype(np.float32),
        "wgt": np.repeat(np.random.uniform(0.5, 2.0, (8, J)), 16, axis=0).astype(np.float32),
        "wg_words": p_wg[0],
        "wg_scales": p_wg[1],
        "wu": (n((K, R)) / np.sqrt(K) / s * u.T).astype(np.float32),
        "wd": (n((R, N)) / np.sqrt(R) / u).astype(np.float32),
        "offs": striped8(np.stack([np.random.permutation(T)[:J] for _ in range(8)])),
    }


def reference(xT, wgt, wg_words, wg_scales, wu, wd, offs):
    idx = unstriped8(offs)
    rows = np.arange(K)
    xg = f64(wgt)[rows // 4 % 128] * f64(xT)[rows[:, None], idx[rows % 512 // 64]]
    xT_ = mxq(xg, 0, "e4m3")
    wg_ = unpack_weight(wg_words, wg_scales, "e2m1")
    wu_ = mxq(f64(wu), 0, "e4m3")
    ga = wg_.T @ xT_
    ub = wu_.T @ xT_
    h = np.maximum(ga, 0.0) * ub
    h_ = mxq(h, 0, "e4m3")
    wd_ = mxq(f64(wd), 0, "e4m3")
    y = wd_.T @ h_
    return y

@@ -1,0 +1,204 @@
+from contextlib import ExitStack
+
+import concourse.mybir as mybir
+
+K, R, N, T, J = 1024, 512, 512, 2048, 1024
+FLOPS = 2 * J * (2 * K * R + R * N)
+
+F32 = mybir.dt.float32
+BF16 = mybir.dt.bfloat16
+I32 = mybir.dt.int32
+U32 = mybir.dt.uint32
+U16 = mybir.dt.uint16
+U8 = mybir.dt.uint8
+FP8X4 = mybir.dt.float8_e4m3fn_x4
+FP4X4 = mybir.dt.float4_e2m1fn_x4
+MULT = mybir.AluOpType.mult
+MAX = mybir.AluOpType.max
+
+P = 128
+PACK = 4
+PASSES = K // (P * PACK)
+HALF = J // 2
+CHUNK = 256
+SUB = 128
+LIST = 16
+
+
+def tile_list_relu_none_kernel(tc, xT, wgt, wg_words, wg_scales, wu, wd, offs, out):
+    nc = tc.nc
+    with ExitStack() as ctx:
+        keep = ctx.enter_context(tc.tile_pool(name="keep", bufs=1))
+        ring = ctx.enter_context(tc.tile_pool(name="ring", bufs=3))
+        psum = ctx.enter_context(tc.psum_pool(name="psum", bufs=3))
+
+        offsets = keep.tile([P, J // LIST], U16, name="offsets")
+        weight = keep.tile([P, J], F32, name="weight")
+        planes = [[keep.tile([P, T], F32, name="x%d%d" % (a, i)) for i in range(PACK)] for a in range(PASSES)]
+        wu_raw = [keep.tile([P, PACK, R], F32, name="wu_raw%d" % a) for a in range(PASSES)]
+        wd_raw = keep.tile([P, PACK, N], F32, name="wd_raw")
+        wg_raw = keep.tile([P, PASSES, 2 * R], U8, name="wg_raw")
+        ws_raw = keep.tile([P, PASSES, R], U8, name="ws_raw")
+        nc.vector.memset(ws_raw[:].bitcast(I32), 0)
+
+        x_rows = xT.rearrange("(a p i) t -> a i p t", a=PASSES, i=PACK)
+        wu_rows = wu.rearrange("(a p i) r -> a p i r", a=PASSES, i=PACK)
+        wd_rows = wd.rearrange("(m t e) n -> e m t n", t=PACK, e=PACK)
+        ws_rows = wg_scales.rearrange("a q r -> q a r")
+
+        nc.sync.dma_start(offsets[:], offs)
+        nc.sync.dma_start(weight[:, :HALF], wgt[:, :HALF])
+        nc.sync.dma_start(planes[0][0][:], x_rows[0, 0])
+        nc.sync.dma_start(weight[:, HALF:], wgt[:, HALF:])
+        for i in range(1, PACK):
+            nc.sync.dma_start(planes[0][i][:], x_rows[0, i])
+        nc.sync.dma_start(wu_raw[0][:], wu_rows[0])
+        nc.sync.dma_start(wg_raw[:].bitcast(I32), wg_words.rearrange("a p b -> p a b").bitcast(I32))
+        for q in range(4):
+            nc.sync.dma_start(ws_raw[32 * q : 32 * q + 4].bitcast(I32), ws_rows[4 * q : 4 * q + 4].bitcast(I32))
+        for i in range(PACK):
+            nc.sync.dma_start(planes[1][i][:], x_rows[1, i])
+        nc.sync.dma_start(wu_raw[1][:], wu_rows[1])
+        for e in range(PACK):
+            nc.sync.dma_start(wd_raw[e:P:PACK], wd_rows[e])
+
+        def gather(dst, a, i, j0, width):
+            cols = slice(j0 // LIST, (j0 + width) // LIST)
+            nc.vector.tensor_tensor(dst, planes[a][i][:].indirect(offsets[:, cols]), weight[:, j0 : j0 + width], MULT)
+
+        def interleave(engine_copy, src, width, name):
+            grouped = keep.tile([P, width * PACK], BF16, name=name, align_bytes=64)
+            engine_copy(
+                grouped[:].rearrange("p (c e i) -> p c i e", e=4, i=PACK),
+                src.rearrange("p i (c e) -> p c i e", e=4),
+            )
+            return grouped
+
+        def quantise(grouped, width, name):
+            codes = keep.tile([P, width], U32, name=name + "_codes", align_bytes=64)
+            scales = keep.tile([P, width], U8, name=name + "_scales", align_bytes=64)
+            nc.vector.quantize_mx(out=codes[:].bitcast(FP8X4), scales=scales[:], in_=grouped[:])
+            return codes, scales
+
+        def cast_wu(engine_copy, a):
+            grouped = keep.tile([P, R * PACK], BF16, name="wu_grouped%d" % a, align_bytes=64)
+            engine_copy(
+                grouped[:].rearrange("p (t m e i) -> p m t i e", t=PACK, e=4, i=PACK),
+                wu_raw[a][:].rearrange("p i (m t e) -> p m t i e", t=PACK, e=4),
+            )
+            return grouped
+
+        chunks = J // CHUNK
+        picked0 = [keep.tile([P, PACK, HALF], F32, name="picked0_%d" % h) for h in range(2)]
+        for i in range(PACK):
+            for h in range(2):
+                gather(picked0[h][:, i, :], 0, i, h * HALF, HALF)
+
+        wu_q = [None, None]
+        wu_grouped0 = cast_wu(nc.scalar.copy, 0)
+        x_grouped0 = []
+        for c in range(chunks):
+            lo = (c % 2) * CHUNK
+            x_grouped0.append(interleave(nc.scalar.copy, picked0[c // 2][:, :, lo : lo + CHUNK], CHUNK, "xg0_%d" % c))
+
+        wg_codes = keep.tile([P, PASSES, 2 * R], U8, name="wg_codes", align_bytes=64)
+        wg_sc = keep.tile([P, PASSES, R], U8, name="wg_sc", align_bytes=64)
+        picked1 = [keep.tile([P, PACK, CHUNK], F32, name="picked1_%d" % c) for c in range(chunks)]
+        xq = [[None] * chunks, [None] * chunks]
+        for c in range(chunks):
+            gather(picked1[c][:, 0, :], 1, 0, c * CHUNK, CHUNK)
+        nc.vector.tensor_copy(
+            wg_codes[:].bitcast(I32).rearrange("p a (t m w) -> p a m t w", t=PACK, w=2),
+            wg_raw[:].bitcast(I32).rearrange("p a (m t w) -> p a m t w", t=PACK, w=2),
+        )
+        nc.vector.tensor_copy(
+            wg_sc[:].bitcast(I32).rearrange("p a (t m) -> p a m t", t=PACK),
+            ws_raw[:].bitcast(I32).rearrange("p a (m t) -> p a m t", t=PACK),
+        )
+        wu_q[0] = quantise(wu_grouped0, R, "wu0")
+        for c in range(chunks):
+            gather(picked1[c][:, 1, :], 1, 1, c * CHUNK, CHUNK)
+        for c in range(chunks):
+            gather(picked1[c][:, 2, :], 1, 2, c * CHUNK, CHUNK)
+            xq[0][c] = quantise(x_grouped0[c], CHUNK, "xq0_%d" % c)
+
+        x_grouped1 = []
+        for c in range(chunks):
+            gather(picked1[c][:, 3, :], 1, 3, c * CHUNK, CHUNK)
+            x_grouped1.append(interleave(nc.scalar.copy, picked1[c][:], CHUNK, "xg1_%d" % c))
+            if c >= 1:
+                xq[1][c - 1] = quantise(x_grouped1[c - 1], CHUNK, "xq1_%d" % (c - 1))
+        wu_grouped1 = cast_wu(nc.vector.tensor_copy, 1)
+        xq[1][chunks - 1] = quantise(x_grouped1[chunks - 1], CHUNK, "xq1_%d" % (chunks - 1))
+        wu_q[1] = quantise(wu_grouped1, R, "wu1")
+        wd_grouped = interleave(nc.vector.tensor_copy, wd_raw[:], N, "wd_grouped")
+
+        def stage1(lhs_codes, lhs_scales, c, s, name):
+            bank = psum.tile([P, PACK, SUB], F32, name=name)
+            cols = slice(s * SUB, (s + 1) * SUB)
+            for a in range(PASSES):
+                codes, scales = xq[a][c]
+                for t in range(PACK):
+                    nc.tensor.matmul_mx(
+                        out=bank[:, t, :],
+                        lhsT=lhs_codes(a, t),
+                        lhsT_scale=lhs_scales(a, t),
+                        rhs=codes[:, cols].bitcast(FP8X4),
+                        rhs_scale=scales[:, cols],
+                        start=(a == 0 and t == 0),
+                        stop=(a == PASSES - 1 and t == PACK - 1),
+                    )
+            return bank
+
+        def gate_half(c, s):
+            bank = stage1(
+                lambda a, t: wg_codes[:, a, 2 * P * t : 2 * P * (t + 1)].bitcast(FP4X4),
+                lambda a, t: wg_sc[:, a, P * t : P * (t + 1)],
+                c, s, "gate_bank")
+            gate = keep.tile([P, SUB, PACK], F32, name="gate%d_%d" % (c, s))
+            nc.scalar.copy(gate[:], bank[:].rearrange("p t j -> p j t"))
+            return gate
+
+        def up_half(c, s, gate, h_grouped):
+            bank = stage1(
+                lambda a, t: wu_q[a][0][:, P * t : P * (t + 1)].bitcast(FP8X4),
+                lambda a, t: wu_q[a][1][:, P * t : P * (t + 1)],
+                c, s, "up_bank")
+            nc.vector.scalar_tensor_tensor(
+                h_grouped[:, s * SUB * PACK : (s + 1) * SUB * PACK].rearrange("p (j t) -> p j t", t=PACK),
+                gate[:], 0.0, bank[:].rearrange("p t j -> p j t"), MAX, MULT)
+
+        out_rows = out.rearrange("(u v p) j -> u p v j", v=2, p=P)
+
+        def stage2(c, hq, wd_q):
+            for u in range(2):
+                bank = psum.tile([P, 2, CHUNK], F32, name="y_bank", bufs=2)
+                for v in range(2):
+                    n0 = (2 * u + v) * P
+                    nc.tensor.matmul_mx(
+                        out=bank[:, v, :],
+                        lhsT=wd_q[0][:, n0 : n0 + P].bitcast(FP8X4),
+                        lhsT_scale=wd_q[1][:, n0 : n0 + P],
+                        rhs=hq[0][:].bitcast(FP8X4),
+                        rhs_scale=hq[1][:],
+                        start=True,
+                        stop=True,
+                    )
+                y = keep.tile([P, 2, CHUNK], F32, name="y%d_%d" % (c, u))
+                nc.scalar.copy(y[:], bank[:])
+                nc.sync.dma_start(out_rows[u, :, :, c * CHUNK : (c + 1) * CHUNK], y[:])
+
+        subs = CHUNK // SUB
+        gates = [[gate_half(c, s) for s in range(subs)] for c in range(chunks)]
+        wd_q = None
+        pending = None
+        for c in range(chunks):
+            h_grouped = ring.tile([P, CHUNK * PACK], BF16, name="h_grouped", align_bytes=64)
+            up_half(c, 0, gates[c][0], h_grouped)
+            if c == 0:
+                wd_q = quantise(wd_grouped, N, "wd")
+            else:
+                stage2(c - 1, quantise(pending, CHUNK, "hq%d" % (c - 1)), wd_q)
+            up_half(c, 1, gates[c][1], h_grouped)
+            pending = h_grouped
+        stage2(chunks - 1, quantise(pending, CHUNK, "hq%d" % (chunks - 1)), wd_q)

@@ -23,6 +23,9 @@ HALF = J // 2
 CHUNK = 256
 SUB = 128
 LIST = 16
+GATE_BANK = [0, 2, 4, 6, 0, 2, 5, 4]
+UP_BANK = [1, 3, 5, 7, 1, 3, 7, 6]
+Y_BANK = [4, 6, 0, 2, 1, 3, 5, 7]
 
 
 def tile_list_relu_none_kernel(tc, xT, wgt, wg_words, wg_scales, wu, wd, offs, out):
@@ -30,13 +33,13 @@ def tile_list_relu_none_kernel(tc, xT, wgt, wg_words, wg_scales, wu, wd, offs, o
     with ExitStack() as ctx:
         keep = ctx.enter_context(tc.tile_pool(name="keep", bufs=1))
         ring = ctx.enter_context(tc.tile_pool(name="ring", bufs=3))
-        psum = ctx.enter_context(tc.psum_pool(name="psum", bufs=3))
+        psum = ctx.enter_context(tc.psum_pool(name="psum", bufs=1))
 
         offsets = keep.tile([P, J // LIST], U16, name="offsets")
         weight = keep.tile([P, J], F32, name="weight")
         planes = [[keep.tile([P, T], F32, name="x%d%d" % (a, i)) for i in range(PACK)] for a in range(PASSES)]
         wu_raw = [keep.tile([P, PACK, R], F32, name="wu_raw%d" % a) for a in range(PASSES)]
-        wd_raw = keep.tile([P, PACK, N], F32, name="wd_raw")
+        wd_raw = keep.tile([P, PACK, N], F32, name="wd_raw", tag="wd_slot", align_bytes=64)
         wg_raw = keep.tile([P, PASSES, 2 * R], U8, name="wg_raw")
         ws_raw = keep.tile([P, PASSES, R], U8, name="ws_raw")
         nc.vector.memset(ws_raw[:].bitcast(I32), 0)
@@ -46,33 +49,65 @@ def tile_list_relu_none_kernel(tc, xT, wgt, wg_words, wg_scales, wu, wd, offs, o
         wd_rows = wd.rearrange("(m t e) n -> e m t n", t=PACK, e=PACK)
         ws_rows = wg_scales.rearrange("a q r -> q a r")
 
+        def load_x(a, i):
+            nc.sync.dma_start(planes[a][i][:], x_rows[a, i])
+
         nc.sync.dma_start(offsets[:], offs)
-        nc.sync.dma_start(weight[:, :HALF], wgt[:, :HALF])
-        nc.sync.dma_start(planes[0][0][:], x_rows[0, 0])
+        load_x(0, 0)
+        nc.scalar.dma_start(weight[:, :HALF], wgt[:, :HALF])
         nc.sync.dma_start(weight[:, HALF:], wgt[:, HALF:])
         for i in range(1, PACK):
-            nc.sync.dma_start(planes[0][i][:], x_rows[0, i])
+            load_x(0, i)
+        load_x(1, 0)
         nc.sync.dma_start(wu_raw[0][:], wu_rows[0])
+        load_x(1, 1)
+        nc.sync.dma_start(wu_raw[1][:], wu_rows[1])
         nc.sync.dma_start(wg_raw[:].bitcast(I32), wg_words.rearrange("a p b -> p a b").bitcast(I32))
         for q in range(4):
             nc.sync.dma_start(ws_raw[32 * q : 32 * q + 4].bitcast(I32), ws_rows[4 * q : 4 * q + 4].bitcast(I32))
-        for i in range(PACK):
-            nc.sync.dma_start(planes[1][i][:], x_rows[1, i])
-        nc.sync.dma_start(wu_raw[1][:], wu_rows[1])
+        load_x(1, 2)
+        load_x(1, 3)
         for e in range(PACK):
             nc.sync.dma_start(wd_raw[e:P:PACK], wd_rows[e])
 
-        def gather(dst, a, i, j0, width):
-            cols = slice(j0 // LIST, (j0 + width) // LIST)
-            nc.vector.tensor_tensor(dst, planes[a][i][:].indirect(offsets[:, cols]), weight[:, j0 : j0 + width], MULT)
+        picked = [keep.tile([P, PACK * J], F32, name="picked%d" % a) for a in range(PASSES)]
+        x_grouped = [keep.tile([P, PACK * J], BF16, name="x_grouped%d" % a, align_bytes=64) for a in range(PASSES)]
+        x_codes = {
+            (0, 0): keep.tile([P, HALF], U32, name="x_codes00", align_bytes=64),
+            (0, 1): keep.tile([P, HALF], U32, name="x_codes01", align_bytes=64),
+            (1, 0): keep.tile([P, HALF], U32, name="x_codes10", align_bytes=64),
+        }
 
-        def interleave(engine_copy, src, width, name):
-            grouped = keep.tile([P, width * PACK], BF16, name=name, align_bytes=64)
+        def codes_of(a, j0, width):
+            return x_codes[a, j0 // HALF][:, j0 % HALF : j0 % HALF + width].bitcast(FP8X4)
+
+        x_scales = [keep.tile([P, J], U8, name="x_scales%d" % a, align_bytes=64) for a in range(PASSES)]
+
+        def gather(a, i, j0, width):
+            cols = slice(j0 // LIST, (j0 + width) // LIST)
+            nc.vector.tensor_tensor(
+                picked[a][:, i * J + j0 : i * J + j0 + width],
+                planes[a][i][:].indirect(offsets[:, cols]),
+                weight[:, j0 : j0 + width],
+                MULT,
+            )
+
+        def interleave(engine_copy, grouped, src):
             engine_copy(
-                grouped[:].rearrange("p (c e i) -> p c i e", e=4, i=PACK),
+                grouped.rearrange("p (c e i) -> p c i e", e=4, i=PACK),
                 src.rearrange("p i (c e) -> p c i e", e=4),
             )
-            return grouped
+
+        def group_x(engine_copy, a, j0, width):
+            src = picked[a][:].rearrange("p (i j) -> p i j", i=PACK)[:, :, j0 : j0 + width]
+            interleave(engine_copy, x_grouped[a][:, PACK * j0 : PACK * (j0 + width)], src)
+
+        def quantise_x(a, j0, width):
+            nc.vector.quantize_mx(
+                out=codes_of(a, j0, width),
+                scales=x_scales[a][:, j0 : j0 + width],
+                in_=x_grouped[a][:, PACK * j0 : PACK * (j0 + width)],
+            )
 
         def quantise(grouped, width, name):
             codes = keep.tile([P, width], U32, name=name + "_codes", align_bytes=64)
@@ -80,33 +115,32 @@ def tile_list_relu_none_kernel(tc, xT, wgt, wg_words, wg_scales, wu, wd, offs, o
             nc.vector.quantize_mx(out=codes[:].bitcast(FP8X4), scales=scales[:], in_=grouped[:])
             return codes, scales
 
-        def cast_wu(engine_copy, a):
+        def cast_wu(a):
             grouped = keep.tile([P, R * PACK], BF16, name="wu_grouped%d" % a, align_bytes=64)
-            engine_copy(
+            nc.scalar.copy(
                 grouped[:].rearrange("p (t m e i) -> p m t i e", t=PACK, e=4, i=PACK),
                 wu_raw[a][:].rearrange("p i (m t e) -> p m t i e", t=PACK, e=4),
             )
             return grouped
 
+        banks = [psum.tile([P, PACK * SUB], F32, name="bank%d" % b) for b in range(8)]
         chunks = J // CHUNK
-        picked0 = [keep.tile([P, PACK, HALF], F32, name="picked0_%d" % h) for h in range(2)]
-        for i in range(PACK):
-            for h in range(2):
-                gather(picked0[h][:, i, :], 0, i, h * HALF, HALF)
+        subs = CHUNK // SUB
 
-        wu_q = [None, None]
-        wu_grouped0 = cast_wu(nc.scalar.copy, 0)
-        x_grouped0 = []
-        for c in range(chunks):
-            lo = (c % 2) * CHUNK
-            x_grouped0.append(interleave(nc.scalar.copy, picked0[c // 2][:, :, lo : lo + CHUNK], CHUNK, "xg0_%d" % c))
-
+        gather(0, 0, 0, HALF)
+        gather(0, 0, HALF, HALF)
+        gather(0, 1, 0, J)
+        gather(0, 2, 0, J)
+        for h in range(2):
+            gather(0, 3, h * HALF, HALF)
+            group_x(nc.scalar.copy, 0, h * HALF, HALF)
+        gather(1, 0, 0, J)
+        quantise_x(0, 0, HALF)
+        gather(1, 1, 0, J)
+        quantise_x(0, HALF, HALF)
+        wu_grouped = [cast_wu(a) for a in range(PASSES)]
         wg_codes = keep.tile([P, PASSES, 2 * R], U8, name="wg_codes", align_bytes=64)
         wg_sc = keep.tile([P, PASSES, R], U8, name="wg_sc", align_bytes=64)
-        picked1 = [keep.tile([P, PACK, CHUNK], F32, name="picked1_%d" % c) for c in range(chunks)]
-        xq = [[None] * chunks, [None] * chunks]
-        for c in range(chunks):
-            gather(picked1[c][:, 0, :], 1, 0, c * CHUNK, CHUNK)
         nc.vector.tensor_copy(
             wg_codes[:].bitcast(I32).rearrange("p a (t m w) -> p a m t w", t=PACK, w=2),
             wg_raw[:].bitcast(I32).rearrange("p a (m t w) -> p a m t w", t=PACK, w=2),
@@ -115,64 +149,46 @@ def tile_list_relu_none_kernel(tc, xT, wgt, wg_words, wg_scales, wu, wd, offs, o
             wg_sc[:].bitcast(I32).rearrange("p a (t m) -> p a m t", t=PACK),
             ws_raw[:].bitcast(I32).rearrange("p a (m t) -> p a m t", t=PACK),
         )
-        wu_q[0] = quantise(wu_grouped0, R, "wu0")
-        for c in range(chunks):
-            gather(picked1[c][:, 1, :], 1, 1, c * CHUNK, CHUNK)
-        for c in range(chunks):
-            gather(picked1[c][:, 2, :], 1, 2, c * CHUNK, CHUNK)
-            xq[0][c] = quantise(x_grouped0[c], CHUNK, "xq0_%d" % c)
+        wu_q = [quantise(wu_grouped[0], R, "wu0")]
+        wu_q.append(quantise(wu_grouped[1], R, "wu1"))
+        gather(1, 2, 0, J)
 
-        x_grouped1 = []
-        for c in range(chunks):
-            gather(picked1[c][:, 3, :], 1, 3, c * CHUNK, CHUNK)
-            x_grouped1.append(interleave(nc.scalar.copy, picked1[c][:], CHUNK, "xg1_%d" % c))
-            if c >= 1:
-                xq[1][c - 1] = quantise(x_grouped1[c - 1], CHUNK, "xq1_%d" % (c - 1))
-        wu_grouped1 = cast_wu(nc.vector.tensor_copy, 1)
-        xq[1][chunks - 1] = quantise(x_grouped1[chunks - 1], CHUNK, "xq1_%d" % (chunks - 1))
-        wu_q[1] = quantise(wu_grouped1, R, "wu1")
-        wd_grouped = interleave(nc.vector.tensor_copy, wd_raw[:], N, "wd_grouped")
-
-        def stage1(lhs_codes, lhs_scales, c, s, name):
-            bank = psum.tile([P, PACK, SUB], F32, name=name)
-            cols = slice(s * SUB, (s + 1) * SUB)
+        def stage1(lhs_codes, lhs_scales, j0, slot):
+            bank = banks[slot][:].rearrange("p (t j) -> p t j", t=PACK)
             for a in range(PASSES):
-                codes, scales = xq[a][c]
                 for t in range(PACK):
                     nc.tensor.matmul_mx(
                         out=bank[:, t, :],
                         lhsT=lhs_codes(a, t),
                         lhsT_scale=lhs_scales(a, t),
-                        rhs=codes[:, cols].bitcast(FP8X4),
-                        rhs_scale=scales[:, cols],
+                        rhs=codes_of(a, j0, SUB),
+                        rhs_scale=x_scales[a][:, j0 : j0 + SUB],
                         start=(a == 0 and t == 0),
                         stop=(a == PASSES - 1 and t == PACK - 1),
                     )
             return bank
 
-        def gate_half(c, s):
-            bank = stage1(
+        def hidden(c, s):
+            j0 = c * CHUNK + s * SUB
+            gate_bank = stage1(
                 lambda a, t: wg_codes[:, a, 2 * P * t : 2 * P * (t + 1)].bitcast(FP4X4),
                 lambda a, t: wg_sc[:, a, P * t : P * (t + 1)],
-                c, s, "gate_bank")
-            gate = keep.tile([P, SUB, PACK], F32, name="gate%d_%d" % (c, s))
-            nc.scalar.copy(gate[:], bank[:].rearrange("p t j -> p j t"))
-            return gate
-
-        def up_half(c, s, gate, h_grouped):
-            bank = stage1(
+                j0, GATE_BANK[c * subs + s])
+            gate = ring.tile([P, SUB, PACK], F32, name="gate")
+            nc.scalar.copy(gate[:], gate_bank.rearrange("p t j -> p j t"))
+            up_bank = stage1(
                 lambda a, t: wu_q[a][0][:, P * t : P * (t + 1)].bitcast(FP8X4),
                 lambda a, t: wu_q[a][1][:, P * t : P * (t + 1)],
-                c, s, "up_bank")
+                j0, UP_BANK[c * subs + s])
             nc.vector.scalar_tensor_tensor(
-                h_grouped[:, s * SUB * PACK : (s + 1) * SUB * PACK].rearrange("p (j t) -> p j t", t=PACK),
-                gate[:], 0.0, bank[:].rearrange("p t j -> p j t"), MAX, MULT)
+                h_piece(c, s).rearrange("p (j t) -> p j t", t=PACK),
+                gate[:], 0.0, up_bank.rearrange("p t j -> p j t"), MAX, MULT)
 
         out_rows = out.rearrange("(u v p) j -> u p v j", v=2, p=P)
 
-        def stage2(c, hq, wd_q):
+        def stage2(c, hq, wd_q, copies):
             for u in range(2):
-                bank = psum.tile([P, 2, CHUNK], F32, name="y_bank", bufs=2)
+                bank = banks[Y_BANK[2 * c + u]][:].rearrange("p (v j) -> p v j", v=2)
                 for v in range(2):
                     n0 = (2 * u + v) * P
                     nc.tensor.matmul_mx(
@@ -185,20 +201,54 @@ def tile_list_relu_none_kernel(tc, xT, wgt, wg_words, wg_scales, wu, wd, offs, o
                         stop=True,
                     )
                 y = keep.tile([P, 2, CHUNK], F32, name="y%d_%d" % (c, u))
-                nc.scalar.copy(y[:], bank[:])
+                copies[u](y[:], bank)
                 nc.sync.dma_start(out_rows[u, :, :, c * CHUNK : (c + 1) * CHUNK], y[:])
 
-        subs = CHUNK // SUB
-        gates = [[gate_half(c, s) for s in range(subs)] for c in range(chunks)]
-        wd_q = None
-        pending = None
-        for c in range(chunks):
-            h_grouped = ring.tile([P, CHUNK * PACK], BF16, name="h_grouped", align_bytes=64)
-            up_half(c, 0, gates[c][0], h_grouped)
-            if c == 0:
-                wd_q = quantise(wd_grouped, N, "wd")
-            else:
-                stage2(c - 1, quantise(pending, CHUNK, "hq%d" % (c - 1)), wd_q)
-            up_half(c, 1, gates[c][1], h_grouped)
-            pending = h_grouped
-        stage2(chunks - 1, quantise(pending, CHUNK, "hq%d" % (chunks - 1)), wd_q)
+        gather(1, 3, 0, CHUNK)
+        gather(1, 3, CHUNK, CHUNK)
+        group_x(nc.vector.tensor_copy, 1, 0, CHUNK)
+        group_x(nc.scalar.copy, 1, CHUNK, CHUNK)
+        gather(1, 3, 2 * CHUNK, CHUNK)
+        quantise_x(1, 0, CHUNK)
+        group_x(nc.scalar.copy, 1, 2 * CHUNK, CHUNK)
+        gather(1, 3, 3 * CHUNK, CHUNK)
+        quantise_x(1, CHUNK, CHUNK)
+        wd_grouped = keep.tile([P, N * PACK], BF16, name="wd_grouped", align_bytes=64)
+        interleave(nc.vector.tensor_copy, wd_grouped[:], wd_raw[:])
+        x_codes[1, 1] = keep.tile([P, HALF], U32, name="x_codes11", tag="wd_slot", align_bytes=64)
+        quantise_x(1, 2 * CHUNK, CHUNK)
+
+        h_first = keep.tile([P, CHUNK * PACK], BF16, name="h_first", align_bytes=64)
+
+        def h_piece(c, s):
+            tile = h_first if c == 0 else wd_grouped
+            return tile[:, s * SUB * PACK : (s + 1) * SUB * PACK]
+
+        hq = [
+            (
+                keep.tile([P, CHUNK], U32, name="h_codes%d" % c, align_bytes=64),
+                keep.tile([P, CHUNK], U8, name="h_scales%d" % c, align_bytes=64),
+            )
+            for c in range(chunks)
+        ]
+
+        def quantise_h(c, s):
+            cols = slice(s * SUB, (s + 1) * SUB)
+            nc.vector.quantize_mx(out=hq[c][0][:, cols].bitcast(FP8X4), scales=hq[c][1][:, cols], in_=h_piece(c, s))
+
+        hidden(0, 0)
+        hidden(0, 1)
+        group_x(nc.scalar.copy, 1, 3 * CHUNK, CHUNK)
+        quantise_h(0, 0)
+        wd_q = quantise(wd_grouped, N, "wd")
+        quantise_x(1, 3 * CHUNK, CHUNK)
+        for c in range(1, chunks):
+            hidden(c, 0)
+            quantise_h(c - 1, 1)
+            hidden(c, 1)
+            quantise_h(c, 0)
+            if c < chunks - 1:
+                stage2(c - 1, hq[c - 1], wd_q, (nc.scalar.copy, nc.scalar.copy))
+        quantise_h(chunks - 1, 1)
+        stage2(chunks - 2, hq[chunks - 2], wd_q, (nc.scalar.copy, nc.vector.tensor_copy))
+        stage2(chunks - 1, hq[chunks - 1], wd_q, (nc.scalar.copy, nc.vector.tensor_copy))

@@ -23,22 +23,18 @@ HALF = J // 2
 CHUNK = 256
 SUB = 128
 LIST = 16
-GATE_BANK = [0, 2, 4, 6, 0, 2, 5, 4]
-UP_BANK = [1, 3, 5, 7, 1, 3, 7, 6]
-Y_BANK = [4, 6, 0, 2, 1, 3, 5, 7]
 
 
 def tile_list_relu_none_kernel(tc, xT, wgt, wg_words, wg_scales, wu, wd, offs, out):
     nc = tc.nc
     with ExitStack() as ctx:
         keep = ctx.enter_context(tc.tile_pool(name="keep", bufs=1))
-        ring = ctx.enter_context(tc.tile_pool(name="ring", bufs=3))
         psum = ctx.enter_context(tc.psum_pool(name="psum", bufs=1))
 
         offsets = keep.tile([P, J // LIST], U16, name="offsets")
         weight = keep.tile([P, J], F32, name="weight")
         planes = [[keep.tile([P, T], F32, name="x%d%d" % (a, i)) for i in range(PACK)] for a in range(PASSES)]
-        wu_raw = [keep.tile([P, PACK, R], F32, name="wu_raw%d" % a) for a in range(PASSES)]
+        wu_raw = [keep.tile([P, PACK, R], F32, name="wu_raw%d" % a, tag="wu_slot%d" % a) for a in range(PASSES)]
         wd_raw = keep.tile([P, PACK, N], F32, name="wd_raw", tag="wd_slot", align_bytes=64)
         wg_raw = keep.tile([P, PASSES, 2 * R], U8, name="wg_raw")
         ws_raw = keep.tile([P, PASSES, R], U8, name="ws_raw")
@@ -54,28 +50,37 @@ def tile_list_relu_none_kernel(tc, xT, wgt, wg_words, wg_scales, wu, wd, offs, o
 
         nc.sync.dma_start(offsets[:], offs)
         load_x(0, 0)
-        nc.scalar.dma_start(weight[:, :HALF], wgt[:, :HALF])
-        nc.sync.dma_start(weight[:, HALF:], wgt[:, HALF:])
+        nc.scalar.dma_start(weight[:, :CHUNK], wgt[:, :CHUNK])
+        nc.sync.dma_start(weight[:, CHUNK:], wgt[:, CHUNK:])
         for i in range(1, PACK):
             load_x(0, i)
         load_x(1, 0)
-        nc.sync.dma_start(wu_raw[0][:], wu_rows[0])
         load_x(1, 1)
-        nc.sync.dma_start(wu_raw[1][:], wu_rows[1])
+        nc.sync.dma_start(wu_raw[0][:], wu_rows[0])
         nc.sync.dma_start(wg_raw[:].bitcast(I32), wg_words.rearrange("a p b -> p a b").bitcast(I32))
         for q in range(4):
             nc.sync.dma_start(ws_raw[32 * q : 32 * q + 4].bitcast(I32), ws_rows[4 * q : 4 * q + 4].bitcast(I32))
         load_x(1, 2)
         load_x(1, 3)
+        nc.sync.dma_start(wu_raw[1][:], wu_rows[1])
         for e in range(PACK):
             nc.sync.dma_start(wd_raw[e:P:PACK], wd_rows[e])
 
         picked = [keep.tile([P, PACK * J], F32, name="picked%d" % a) for a in range(PASSES)]
-        x_grouped = [keep.tile([P, PACK * J], BF16, name="x_grouped%d" % a, align_bytes=64) for a in range(PASSES)]
+        x_grouped = [
+            keep.tile([P, PACK * J], BF16, name="x_grouped0", align_bytes=64),
+            keep.tile([P, PACK * HALF], BF16, name="x_grouped1", align_bytes=64),
+        ]
+
+        def grouped_of(a, j0, width):
+            first = j0 if a == 0 else j0 % HALF
+            return x_grouped[a][:, PACK * first : PACK * (first + width)]
+
         x_codes = {
             (0, 0): keep.tile([P, HALF], U32, name="x_codes00", align_bytes=64),
             (0, 1): keep.tile([P, HALF], U32, name="x_codes01", align_bytes=64),
             (1, 0): keep.tile([P, HALF], U32, name="x_codes10", align_bytes=64),
+            (1, 1): keep.tile([P, HALF], U32, name="x_codes11", align_bytes=64),
         }
 
         def codes_of(a, j0, width):
@@ -100,13 +105,13 @@ def tile_list_relu_none_kernel(tc, xT, wgt, wg_words, wg_scales, wu, wd, offs, o
 
         def group_x(engine_copy, a, j0, width):
             src = picked[a][:].rearrange("p (i j) -> p i j", i=PACK)[:, :, j0 : j0 + width]
-            interleave(engine_copy, x_grouped[a][:, PACK * j0 : PACK * (j0 + width)], src)
+            interleave(engine_copy, grouped_of(a, j0, width), src)
 
         def quantise_x(a, j0, width):
             nc.vector.quantize_mx(
                 out=codes_of(a, j0, width),
                 scales=x_scales[a][:, j0 : j0 + width],
-                in_=x_grouped[a][:, PACK * j0 : PACK * (j0 + width)],
+                in_=grouped_of(a, j0, width),
             )
 
         def quantise(grouped, width, name):
@@ -127,18 +132,17 @@ def tile_list_relu_none_kernel(tc, xT, wgt, wg_words, wg_scales, wu, wd, offs, o
         chunks = J // CHUNK
         subs = CHUNK // SUB
 
-        gather(0, 0, 0, HALF)
-        gather(0, 0, HALF, HALF)
+        gather(0, 0, 0, CHUNK)
+        gather(0, 0, CHUNK, J - CHUNK)
         gather(0, 1, 0, J)
         gather(0, 2, 0, J)
         for h in range(2):
             gather(0, 3, h * HALF, HALF)
             group_x(nc.scalar.copy, 0, h * HALF, HALF)
         gather(1, 0, 0, J)
-        quantise_x(0, 0, HALF)
         gather(1, 1, 0, J)
+        quantise_x(0, 0, HALF)
         quantise_x(0, HALF, HALF)
-        wu_grouped = [cast_wu(a) for a in range(PASSES)]
         wg_codes = keep.tile([P, PASSES, 2 * R], U8, name="wg_codes", align_bytes=64)
         wg_sc = keep.tile([P, PASSES, R], U8, name="wg_sc", align_bytes=64)
         nc.vector.tensor_copy(
@@ -149,9 +153,9 @@ def tile_list_relu_none_kernel(tc, xT, wgt, wg_words, wg_scales, wu, wd, offs, o
             wg_sc[:].bitcast(I32).rearrange("p a (t m) -> p a m t", t=PACK),
             ws_raw[:].bitcast(I32).rearrange("p a (m t) -> p a m t", t=PACK),
         )
-        wu_q = [quantise(wu_grouped[0], R, "wu0")]
-        wu_q.append(quantise(wu_grouped[1], R, "wu1"))
+        wu_grouped = [cast_wu(0)]
         gather(1, 2, 0, J)
+        wu_q = [quantise(wu_grouped[0], R, "wu0")]
 
         def stage1(lhs_codes, lhs_scales, j0, slot):
             bank = banks[slot][:].rearrange("p (t j) -> p t j", t=PACK)
@@ -173,52 +177,51 @@ def tile_list_relu_none_kernel(tc, xT, wgt, wg_words, wg_scales, wu, wd, offs, o
             gate_bank = stage1(
                 lambda a, t: wg_codes[:, a, 2 * P * t : 2 * P * (t + 1)].bitcast(FP4X4),
                 lambda a, t: wg_sc[:, a, P * t : P * (t + 1)],
-                j0, GATE_BANK[c * subs + s])
-            gate = ring.tile([P, SUB, PACK], F32, name="gate")
-            nc.scalar.copy(gate[:], gate_bank.rearrange("p t j -> p j t"))
+                j0, c * subs + s)
+            gate = gates[:, PACK * j0 : PACK * (j0 + SUB)].rearrange("p (j t) -> p j t", t=PACK)
+            nc.scalar.copy(gate, gate_bank.rearrange("p t j -> p j t"))
             up_bank = stage1(
                 lambda a, t: wu_q[a][0][:, P * t : P * (t + 1)].bitcast(FP8X4),
                 lambda a, t: wu_q[a][1][:, P * t : P * (t + 1)],
-                j0, UP_BANK[c * subs + s])
+                j0, c * subs + s)
             nc.vector.scalar_tensor_tensor(
                 h_piece(c, s).rearrange("p (j t) -> p j t", t=PACK),
-                gate[:], 0.0, up_bank.rearrange("p t j -> p j t"), MAX, MULT)
+                gate, 0.0, up_bank.rearrange("p t j -> p j t"), MAX, MULT)
 
-        out_rows = out.rearrange("(u v p) j -> u p v j", v=2, p=P)
+        out_rows = out.rearrange("(v p) j -> p v j", p=P)
 
-        def stage2(c, hq, wd_q, copies):
-            for u in range(2):
-                bank = banks[Y_BANK[2 * c + u]][:].rearrange("p (v j) -> p v j", v=2)
-                for v in range(2):
-                    n0 = (2 * u + v) * P
-                    nc.tensor.matmul_mx(
-                        out=bank[:, v, :],
-                        lhsT=wd_q[0][:, n0 : n0 + P].bitcast(FP8X4),
-                        lhsT_scale=wd_q[1][:, n0 : n0 + P],
-                        rhs=hq[0][:].bitcast(FP8X4),
-                        rhs_scale=hq[1][:],
-                        start=True,
-                        stop=True,
-                    )
-                y = keep.tile([P, 2, CHUNK], F32, name="y%d_%d" % (c, u))
-                copies[u](y[:], bank)
-                nc.sync.dma_start(out_rows[u, :, :, c * CHUNK : (c + 1) * CHUNK], y[:])
+        def stage2(c, j0, width, v0, count, slot, copy):
+            bank = banks[slot][:, : count * width].rearrange("p (v j) -> p v j", v=count)
+            for v in range(count):
+                n0 = (v0 + v) * P
+                nc.tensor.matmul_mx(
+                    out=bank[:, v, :],
+                    lhsT=wd_q[0][:, n0 : n0 + P].bitcast(FP8X4),
+                    lhsT_scale=wd_q[1][:, n0 : n0 + P],
+                    rhs=hq[c][0][:, j0 : j0 + width].bitcast(FP8X4),
+                    rhs_scale=hq[c][1][:, j0 : j0 + width],
+                    start=True,
+                    stop=True,
+                )
+            y = keep.tile([P, count, width], F32, name="y%d_%d_%d" % (c, j0, v0))
+            copy(y[:], bank)
+            first = c * CHUNK + j0
+            nc.sync.dma_start(out_rows[:, v0 : v0 + count, first : first + width], y[:])
 
-        gather(1, 3, 0, CHUNK)
-        gather(1, 3, CHUNK, CHUNK)
-        group_x(nc.vector.tensor_copy, 1, 0, CHUNK)
-        group_x(nc.scalar.copy, 1, CHUNK, CHUNK)
-        gather(1, 3, 2 * CHUNK, CHUNK)
-        quantise_x(1, 0, CHUNK)
-        group_x(nc.scalar.copy, 1, 2 * CHUNK, CHUNK)
-        gather(1, 3, 3 * CHUNK, CHUNK)
-        quantise_x(1, CHUNK, CHUNK)
+        for c in range(chunks):
+            gather(1, 3, c * CHUNK, CHUNK)
+            if c < 2:
+                group_x(nc.scalar.copy, 1, c * CHUNK, CHUNK)
+        for c in range(2):
+            quantise_x(1, c * CHUNK, CHUNK)
+            group_x(nc.vector.tensor_copy, 1, (c + 2) * CHUNK, CHUNK)
+        quantise_x(1, 2 * CHUNK, CHUNK)
+        quantise_x(1, 3 * CHUNK, CHUNK)
+        wu_q.append(quantise(cast_wu(1), R, "wu1"))
+        gates = keep.tile([P, PACK * J], F32, name="gates", tag="wu_slot1")
         wd_grouped = keep.tile([P, N * PACK], BF16, name="wd_grouped", align_bytes=64)
         interleave(nc.vector.tensor_copy, wd_grouped[:], wd_raw[:])
-        x_codes[1, 1] = keep.tile([P, HALF], U32, name="x_codes11", tag="wd_slot", align_bytes=64)
-        quantise_x(1, 2 * CHUNK, CHUNK)
-
-        h_first = keep.tile([P, CHUNK * PACK], BF16, name="h_first", align_bytes=64)
+        h_first = keep.tile([P, CHUNK * PACK], BF16, name="h_first", tag="wd_slot", align_bytes=64)
 
         def h_piece(c, s):
             tile = h_first if c == 0 else wd_grouped
@@ -237,18 +240,20 @@ def tile_list_relu_none_kernel(tc, xT, wgt, wg_words, wg_scales, wu, wd, offs, o
             nc.vector.quantize_mx(out=hq[c][0][:, cols].bitcast(FP8X4), scales=hq[c][1][:, cols], in_=h_piece(c, s))
 
         hidden(0, 0)
-        hidden(0, 1)
-        group_x(nc.scalar.copy, 1, 3 * CHUNK, CHUNK)
-        quantise_h(0, 0)
         wd_q = quantise(wd_grouped, N, "wd")
-        quantise_x(1, 3 * CHUNK, CHUNK)
+        hidden(0, 1)
+        quantise_h(0, 0)
         for c in range(1, chunks):
             hidden(c, 0)
             quantise_h(c - 1, 1)
             hidden(c, 1)
             quantise_h(c, 0)
             if c < chunks - 1:
-                stage2(c - 1, hq[c - 1], wd_q, (nc.scalar.copy, nc.scalar.copy))
-        quantise_h(chunks - 1, 1)
-        stage2(chunks - 2, hq[chunks - 2], wd_q, (nc.scalar.copy, nc.vector.tensor_copy))
-        stage2(chunks - 1, hq[chunks - 1], wd_q, (nc.scalar.copy, nc.vector.tensor_copy))
+                for u in range(2):
+                    stage2(c - 1, 0, CHUNK, 2 * u, 2, 2 * (c - 1) + u, nc.scalar.copy)
+        quantise_h(3, 1)
+        stage2(2, 0, CHUNK, 0, 2, 4, nc.scalar.copy)
+        stage2(2, 0, CHUNK, 2, 2, 5, nc.scalar.copy)
+        stage2(3, 0, SUB, 0, 4, 6, nc.vector.tensor_copy)
+        stage2(3, SUB, SUB, 0, 2, 0, nc.vector.tensor_copy)
+        stage2(3, SUB, SUB, 2, 2, 1, nc.scalar.copy)

@@ -1,6 +1,7 @@
 from contextlib import ExitStack
 
 import concourse.mybir as mybir
+from concourse.masks import make_identity
 
 K, R, N, T, J = 1024, 512, 512, 2048, 1024
 FLOPS = 2 * J * (2 * K * R + R * N)
@@ -23,6 +24,10 @@ HALF = J // 2
 CHUNK = 256
 SUB = 128
 LIST = 16
+RUN = 4
+HEADS = 8
+BLOCKS = J // P
+EARLY = 2
 
 
 def tile_list_relu_none_kernel(tc, xT, wgt, wg_words, wg_scales, wu, wd, offs, out):
@@ -31,27 +36,36 @@ def tile_list_relu_none_kernel(tc, xT, wgt, wg_words, wg_scales, wu, wd, offs, o
         keep = ctx.enter_context(tc.tile_pool(name="keep", bufs=1))
         psum = ctx.enter_context(tc.psum_pool(name="psum", bufs=1))
 
+        def tile(name, width, dtype):
+            return keep.tile([P, width], dtype, name=name, align_bytes=64)
+
         offsets = keep.tile([P, J // LIST], U16, name="offsets")
-        weight = keep.tile([P, J], F32, name="weight")
-        planes = [[keep.tile([P, T], F32, name="x%d%d" % (a, i)) for i in range(PACK)] for a in range(PASSES)]
-        wu_raw = [keep.tile([P, PACK, R], F32, name="wu_raw%d" % a, tag="wu_slot%d" % a) for a in range(PASSES)]
-        wd_raw = keep.tile([P, PACK, N], F32, name="wd_raw", tag="wd_slot", align_bytes=64)
+        weight = tile("weight", J, F32)
+        planes = [
+            [keep.tile([P, T], F32, name="x%d%d" % (a, i), tag="plane%d%d" % (a, i), align_bytes=64) for i in range(PACK)]
+            for a in range(PASSES)
+        ]
+        wu_raw = [keep.tile([P, PACK, R], F32, name="wu_raw%d" % a, tag="slot%d" % a, align_bytes=64) for a in range(PASSES)]
+        wd_raw = keep.tile([P, PACK, N], F32, name="wd_raw", tag="slot_wd", align_bytes=64)
         wg_raw = keep.tile([P, PASSES, 2 * R], U8, name="wg_raw")
         ws_raw = keep.tile([P, PASSES, R], U8, name="ws_raw")
         nc.vector.memset(ws_raw[:].bitcast(I32), 0)
 
         x_rows = xT.rearrange("(a p i) t -> a i p t", a=PASSES, i=PACK)
         wu_rows = wu.rearrange("(a p i) r -> a p i r", a=PASSES, i=PACK)
-        wd_rows = wd.rearrange("(m t e) n -> e m t n", t=PACK, e=PACK)
+        wd_rows = wd.rearrange("(m t e) n -> t m e n", t=PACK, e=RUN)
         ws_rows = wg_scales.rearrange("a q r -> q a r")
 
         def load_x(a, i):
             nc.sync.dma_start(planes[a][i][:], x_rows[a, i])
 
+        head_rows = tile("head_rows", P, F32)
+        nc.vector.memset(head_rows[HEADS * BLOCKS :, :], 0.0)
+        nc.scalar.dma_start(head_rows[: HEADS * BLOCKS, :], wgt.rearrange("(g r) (b c) -> r g b c", r=LIST, c=P)[0])
+        identity = tile("identity", P, F32)
+        make_identity(nc, identity[:])
         nc.sync.dma_start(offsets[:], offs)
         load_x(0, 0)
-        nc.scalar.dma_start(weight[:, :CHUNK], wgt[:, :CHUNK])
-        nc.sync.dma_start(weight[:, CHUNK:], wgt[:, CHUNK:])
         for i in range(1, PACK):
             load_x(0, i)
         load_x(1, 0)
@@ -63,30 +77,21 @@ def tile_list_relu_none_kernel(tc, xT, wgt, wg_words, wg_scales, wu, wd, offs, o
         load_x(1, 2)
         load_x(1, 3)
         nc.sync.dma_start(wu_raw[1][:], wu_rows[1])
-        for e in range(PACK):
-            nc.sync.dma_start(wd_raw[e:P:PACK], wd_rows[e])
+        for t in range(PACK):
+            nc.sync.dma_start(wd_raw[:, t, :], wd_rows[t])
 
-        picked = [keep.tile([P, PACK * J], F32, name="picked%d" % a) for a in range(PASSES)]
-        x_grouped = [
-            keep.tile([P, PACK * J], BF16, name="x_grouped0", align_bytes=64),
-            keep.tile([P, PACK * HALF], BF16, name="x_grouped1", align_bytes=64),
-        ]
+        wg_codes = keep.tile([P, PASSES, 2 * R], U8, name="wg_codes", align_bytes=64)
+        wg_sc = keep.tile([P, PASSES, R], U8, name="wg_sc", align_bytes=64)
+        nc.vector.tensor_copy(
+            wg_sc[:].bitcast(I32).rearrange("p a (t m) -> p a m t", t=PACK),
+            ws_raw[:].bitcast(I32).rearrange("p a (m t) -> p a m t", t=PACK),
+        )
 
-        def grouped_of(a, j0, width):
-            first = j0 if a == 0 else j0 % HALF
-            return x_grouped[a][:, PACK * first : PACK * (first + width)]
-
-        x_codes = {
-            (0, 0): keep.tile([P, HALF], U32, name="x_codes00", align_bytes=64),
-            (0, 1): keep.tile([P, HALF], U32, name="x_codes01", align_bytes=64),
-            (1, 0): keep.tile([P, HALF], U32, name="x_codes10", align_bytes=64),
-            (1, 1): keep.tile([P, HALF], U32, name="x_codes11", align_bytes=64),
-        }
-
-        def codes_of(a, j0, width):
-            return x_codes[a, j0 // HALF][:, j0 % HALF : j0 % HALF + width].bitcast(FP8X4)
-
-        x_scales = [keep.tile([P, J], U8, name="x_scales%d" % a, align_bytes=64) for a in range(PASSES)]
+        picked = [tile("picked%d" % a, PACK * J, F32) for a in range(PASSES)]
+        widths = [J, CHUNK]
+        x_grouped = [[tile("x_grouped0", PACK * J, BF16)]]
+        x_codes = [[], [tile("x_codes1_%d" % c, CHUNK, U32) for c in range(2)]]
+        x_scales = [[tile("x_scales%d_%d" % (a, c), widths[a], U8) for c in range(J // widths[a])] for a in range(PASSES)]
 
         def gather(a, i, j0, width):
             cols = slice(j0 // LIST, (j0 + width) // LIST)
@@ -103,90 +108,90 @@ def tile_list_relu_none_kernel(tc, xT, wgt, wg_words, wg_scales, wu, wd, offs, o
                 src.rearrange("p i (c e) -> p c i e", e=4),
             )
 
-        def group_x(engine_copy, a, j0, width):
-            src = picked[a][:].rearrange("p (i j) -> p i j", i=PACK)[:, :, j0 : j0 + width]
-            interleave(engine_copy, grouped_of(a, j0, width), src)
+        def group_first(j0, width):
+            src = picked[0][:].rearrange("p (i j) -> p i j", i=PACK)[:, :, j0 : j0 + width]
+            interleave(nc.scalar.copy, x_grouped[0][0][:, PACK * j0 : PACK * (j0 + width)], src)
 
-        def quantise_x(a, j0, width):
-            nc.vector.quantize_mx(
-                out=codes_of(a, j0, width),
-                scales=x_scales[a][:, j0 : j0 + width],
-                in_=grouped_of(a, j0, width),
-            )
-
-        def quantise(grouped, width, name):
-            codes = keep.tile([P, width], U32, name=name + "_codes", align_bytes=64)
-            scales = keep.tile([P, width], U8, name=name + "_scales", align_bytes=64)
-            nc.vector.quantize_mx(out=codes[:].bitcast(FP8X4), scales=scales[:], in_=grouped[:])
-            return codes, scales
-
-        def cast_wu(a):
-            grouped = keep.tile([P, R * PACK], BF16, name="wu_grouped%d" % a, align_bytes=64)
+        def group_pair(c, i0):
+            src = picked[1][:].rearrange("p (i j) -> p i j", i=PACK)[:, i0 : i0 + 2, c * CHUNK : (c + 1) * CHUNK]
             nc.scalar.copy(
-                grouped[:].rearrange("p (t m e i) -> p m t i e", t=PACK, e=4, i=PACK),
-                wu_raw[a][:].rearrange("p i (m t e) -> p m t i e", t=PACK, e=4),
+                x_grouped[1][c].rearrange("p (c e i) -> p c i e", e=4, i=PACK)[:, :, i0 : i0 + 2, :],
+                src.rearrange("p i (c e) -> p c i e", e=4),
             )
-            return grouped
+
+        def quantise(codes, scales, grouped):
+            nc.vector.quantize_mx(out=codes.bitcast(FP8X4), scales=scales, in_=grouped)
+
+        def quantise_x(a, c):
+            quantise(x_codes[a][c][:, :], x_scales[a][c][:], x_grouped[a][c][:, :])
+
+        wu_grouped = [tile("wu_grouped%d" % a, R * PACK, BF16) for a in range(PASSES)]
+        wu_codes = [tile("wu_codes%d" % a, R, U32) for a in range(PASSES)]
+        wu_scales = [tile("wu_scales%d" % a, R, U8) for a in range(PASSES)]
+
+        def cast_wu(engine_copy, a):
+            engine_copy(
+                wu_grouped[a][:].rearrange("p (t m e i) -> p m t i e", t=PACK, e=RUN, i=PACK),
+                wu_raw[a][:].rearrange("p i (m t e) -> p m t i e", t=PACK, e=RUN),
+            )
+
+        def quantise_wu(a):
+            quantise(wu_codes[a][:], wu_scales[a][:], wu_grouped[a][:])
+
+        wd_grouped = tile("wd_grouped", N * PACK, BF16)
+        wd_codes = tile("wd_codes", N, U32)
+        wd_scales = tile("wd_scales", N, U8)
 
         banks = [psum.tile([P, PACK * SUB], F32, name="bank%d" % b) for b in range(8)]
         chunks = J // CHUNK
-        subs = CHUNK // SUB
+        pieces = J // SUB
+        gates = [tile("gate%d" % s, PACK * SUB, F32) for s in range(pieces)]
+        h_grouped = []
+        h_codes = [tile("h_codes%d" % c, CHUNK, U32) for c in range(chunks)]
+        h_scales = [tile("h_scales%d" % c, CHUNK, U8) for c in range(chunks)]
 
-        gather(0, 0, 0, CHUNK)
-        gather(0, 0, CHUNK, J - CHUNK)
-        gather(0, 1, 0, J)
-        gather(0, 2, 0, J)
-        for h in range(2):
-            gather(0, 3, h * HALF, HALF)
-            group_x(nc.scalar.copy, 0, h * HALF, HALF)
-        gather(1, 0, 0, J)
-        gather(1, 1, 0, J)
-        quantise_x(0, 0, HALF)
-        quantise_x(0, HALF, HALF)
-        wg_codes = keep.tile([P, PASSES, 2 * R], U8, name="wg_codes", align_bytes=64)
-        wg_sc = keep.tile([P, PASSES, R], U8, name="wg_sc", align_bytes=64)
-        nc.vector.tensor_copy(
-            wg_codes[:].bitcast(I32).rearrange("p a (t m w) -> p a m t w", t=PACK, w=2),
-            wg_raw[:].bitcast(I32).rearrange("p a (m t w) -> p a m t w", t=PACK, w=2),
-        )
-        nc.vector.tensor_copy(
-            wg_sc[:].bitcast(I32).rearrange("p a (t m) -> p a m t", t=PACK),
-            ws_raw[:].bitcast(I32).rearrange("p a (m t) -> p a m t", t=PACK),
-        )
-        wu_grouped = [cast_wu(0)]
-        gather(1, 2, 0, J)
-        wu_q = [quantise(wu_grouped[0], R, "wu0")]
+        def stage1(lhs_codes, lhs_scales, s, a, first, last):
+            bank = banks[s][:].rearrange("p (t j) -> p t j", t=PACK)
+            c, j0 = divmod(s * SUB, widths[a])
+            for t in range(PACK):
+                nc.tensor.matmul_mx(
+                    out=bank[:, t, :],
+                    lhsT=lhs_codes(a, t),
+                    lhsT_scale=lhs_scales(a, t),
+                    rhs=x_codes[a][c][:, j0 : j0 + SUB].bitcast(FP8X4),
+                    rhs_scale=x_scales[a][c][:, j0 : j0 + SUB],
+                    start=(first and t == 0),
+                    stop=(last and t == PACK - 1),
+                )
 
-        def stage1(lhs_codes, lhs_scales, j0, slot):
-            bank = banks[slot][:].rearrange("p (t j) -> p t j", t=PACK)
-            for a in range(PASSES):
-                for t in range(PACK):
-                    nc.tensor.matmul_mx(
-                        out=bank[:, t, :],
-                        lhsT=lhs_codes(a, t),
-                        lhsT_scale=lhs_scales(a, t),
-                        rhs=codes_of(a, j0, SUB),
-                        rhs_scale=x_scales[a][:, j0 : j0 + SUB],
-                        start=(a == 0 and t == 0),
-                        stop=(a == PASSES - 1 and t == PACK - 1),
-                    )
-            return bank
-
-        def hidden(c, s):
-            j0 = c * CHUNK + s * SUB
-            gate_bank = stage1(
+        def gate_pass(s, a):
+            stage1(
                 lambda a, t: wg_codes[:, a, 2 * P * t : 2 * P * (t + 1)].bitcast(FP4X4),
                 lambda a, t: wg_sc[:, a, P * t : P * (t + 1)],
-                j0, c * subs + s)
-            gate = gates[:, PACK * j0 : PACK * (j0 + SUB)].rearrange("p (j t) -> p j t", t=PACK)
-            nc.scalar.copy(gate, gate_bank.rearrange("p t j -> p j t"))
-            up_bank = stage1(
-                lambda a, t: wu_q[a][0][:, P * t : P * (t + 1)].bitcast(FP8X4),
-                lambda a, t: wu_q[a][1][:, P * t : P * (t + 1)],
-                j0, c * subs + s)
+                s, a, a == 0, a == 1)
+
+        def by_token(s):
+            return banks[s][:].rearrange("p (t j) -> p j t", t=PACK)
+
+        def gate(s):
+            gate_pass(s, 1)
+            nc.scalar.copy(gates[s][:].rearrange("p (j t) -> p j t", t=PACK), by_token(s))
+
+        def hidden(s):
+            order = (0, 1) if s < EARLY else (1, 0)
+            for a in order:
+                stage1(
+                    lambda a, t: wu_codes[a][:, P * t : P * (t + 1)].bitcast(FP8X4),
+                    lambda a, t: wu_scales[a][:, P * t : P * (t + 1)],
+                    s, a, a == order[0], a == order[1])
+            c, j0 = divmod(s * SUB, CHUNK)
             nc.vector.scalar_tensor_tensor(
-                h_piece(c, s).rearrange("p (j t) -> p j t", t=PACK),
-                gate, 0.0, up_bank.rearrange("p t j -> p j t"), MAX, MULT)
+                h_grouped[c][:, PACK * j0 : PACK * (j0 + SUB)].rearrange("p (j t) -> p j t", t=PACK),
+                gates[s][:].rearrange("p (j t) -> p j t", t=PACK), 0.0, by_token(s), MAX, MULT)
+
+        def quantise_h(c, j0, width):
+            quantise(h_codes[c][:, j0 : j0 + width], h_scales[c][:, j0 : j0 + width],
+                     h_grouped[c][:, PACK * j0 : PACK * (j0 + width)])
 
         out_rows = out.rearrange("(v p) j -> p v j", p=P)
 
@@ -196,10 +201,10 @@ def tile_list_relu_none_kernel(tc, xT, wgt, wg_words, wg_scales, wu, wd, offs, o
                 n0 = (v0 + v) * P
                 nc.tensor.matmul_mx(
                     out=bank[:, v, :],
-                    lhsT=wd_q[0][:, n0 : n0 + P].bitcast(FP8X4),
-                    lhsT_scale=wd_q[1][:, n0 : n0 + P],
-                    rhs=hq[c][0][:, j0 : j0 + width].bitcast(FP8X4),
-                    rhs_scale=hq[c][1][:, j0 : j0 + width],
+                    lhsT=wd_codes[:, n0 : n0 + P].bitcast(FP8X4),
+                    lhsT_scale=wd_scales[:, n0 : n0 + P],
+                    rhs=h_codes[c][:, j0 : j0 + width].bitcast(FP8X4),
+                    rhs_scale=h_scales[c][:, j0 : j0 + width],
                     start=True,
                     stop=True,
                 )
@@ -208,52 +213,93 @@ def tile_list_relu_none_kernel(tc, xT, wgt, wg_words, wg_scales, wu, wd, offs, o
             first = c * CHUNK + j0
             nc.sync.dma_start(out_rows[:, v0 : v0 + count, first : first + width], y[:])
 
+        def result(c, u):
+            stage2(c, 0, CHUNK, 2 * u, 2, 2 * c + u, nc.scalar.copy)
+
+        parts = [(0, CHUNK, nc.vector.tensor_copy), (J - CHUNK, CHUNK, nc.vector.tensor_copy), (CHUNK, HALF, nc.scalar.copy)]
+        for bank in (banks[3], banks[4]):
+            nc.tensor.transpose(bank[:, :P], head_rows[:], identity[:])
+        for n, (j0, width, copy) in enumerate(parts):
+            b0, count = j0 // P, width // P
+            by_block = banks[3 + n // 2][:, : HEADS * BLOCKS].rearrange("p (g b) -> p b g", b=BLOCKS)
+            spread = keep.tile([P, count, HEADS, LIST], F32, name="spread%d" % n)
+            copy(spread[:], by_block[:, b0 : b0 + count, :].unsqueeze(3).to_broadcast([P, count, HEADS, LIST]))
+            for b in range(count):
+                nc.tensor.transpose(banks[n][:, P * b : P * (b + 1)], spread[:, b].rearrange("p g r -> p (g r)"), identity[:])
+        for n, (j0, width, copy) in enumerate(parts):
+            copy = nc.vector.tensor_copy if n == 0 else nc.scalar.copy
+            copy(weight[:, j0 : j0 + width], banks[n][:, :width])
+        for j0, width, copy in parts:
+            gather(0, 0, j0, width)
+        gather(0, 1, 0, J)
+        gather(0, 2, 0, J)
+        for h in range(2):
+            gather(0, 3, h * HALF, HALF)
+            group_first(h * HALF, HALF)
+        gather(1, 0, 0, J)
+        gather(1, 1, 0, J)
+        x_codes[0].append(keep.tile([P, J], U32, name="x_codes0", tag="plane11", align_bytes=64))
+        quantise_x(0, 0)
+        nc.vector.tensor_copy(
+            wg_codes[:].bitcast(I32).rearrange("p a (t m w) -> p a m t w", t=PACK, w=2),
+            wg_raw[:].bitcast(I32).rearrange("p a (m t w) -> p a m t w", t=PACK, w=2),
+        )
+        cast_wu(nc.scalar.copy, 0)
+        quantise_wu(0)
+        grouped1 = keep.tile([P, PACK * J], BF16, name="x_grouped1", tag="slot0", align_bytes=64)
+        x_grouped.append([grouped1[:, PACK * c * CHUNK : PACK * (c + 1) * CHUNK] for c in range(chunks)])
+        for c in range(chunks):
+            group_pair(c, 0)
+        gather(1, 2, 0, J)
+        for s in range(pieces):
+            gate_pass(s, 0)
+
         for c in range(chunks):
             gather(1, 3, c * CHUNK, CHUNK)
-            if c < 2:
-                group_x(nc.scalar.copy, 1, c * CHUNK, CHUNK)
-        for c in range(2):
-            quantise_x(1, c * CHUNK, CHUNK)
-            group_x(nc.vector.tensor_copy, 1, (c + 2) * CHUNK, CHUNK)
-        quantise_x(1, 2 * CHUNK, CHUNK)
-        quantise_x(1, 3 * CHUNK, CHUNK)
-        wu_q.append(quantise(cast_wu(1), R, "wu1"))
-        gates = keep.tile([P, PACK * J], F32, name="gates", tag="wu_slot1")
-        wd_grouped = keep.tile([P, N * PACK], BF16, name="wd_grouped", align_bytes=64)
+        group_pair(0, 2)
+        group_pair(1, 2)
+        group_pair(2, 2)
+        group_pair(3, 2)
+        quantise_x(1, 0)
+        quantise_x(1, 1)
+        cast_wu(nc.vector.tensor_copy, 1)
+        late = keep.tile([P, 2 * CHUNK], U32, name="late_codes", tag="slot1", align_bytes=64)
+        x_codes[1].extend([late[:, :CHUNK], late[:, CHUNK:]])
+        gate(0)
+        gate(1)
+        gate(2)
+        gate(3)
+        quantise_x(1, 2)
+        quantise_x(1, 3)
+        quantise_wu(1)
         interleave(nc.vector.tensor_copy, wd_grouped[:], wd_raw[:])
-        h_first = keep.tile([P, CHUNK * PACK], BF16, name="h_first", tag="wd_slot", align_bytes=64)
-
-        def h_piece(c, s):
-            tile = h_first if c == 0 else wd_grouped
-            return tile[:, s * SUB * PACK : (s + 1) * SUB * PACK]
-
-        hq = [
-            (
-                keep.tile([P, CHUNK], U32, name="h_codes%d" % c, align_bytes=64),
-                keep.tile([P, CHUNK], U8, name="h_scales%d" % c, align_bytes=64),
-            )
-            for c in range(chunks)
-        ]
-
-        def quantise_h(c, s):
-            cols = slice(s * SUB, (s + 1) * SUB)
-            nc.vector.quantize_mx(out=hq[c][0][:, cols].bitcast(FP8X4), scales=hq[c][1][:, cols], in_=h_piece(c, s))
-
-        hidden(0, 0)
-        wd_q = quantise(wd_grouped, N, "wd")
-        hidden(0, 1)
-        quantise_h(0, 0)
-        for c in range(1, chunks):
-            hidden(c, 0)
-            quantise_h(c - 1, 1)
-            hidden(c, 1)
-            quantise_h(c, 0)
-            if c < chunks - 1:
-                for u in range(2):
-                    stage2(c - 1, 0, CHUNK, 2 * u, 2, 2 * (c - 1) + u, nc.scalar.copy)
-        quantise_h(3, 1)
-        stage2(2, 0, CHUNK, 0, 2, 4, nc.scalar.copy)
-        stage2(2, 0, CHUNK, 2, 2, 5, nc.scalar.copy)
-        stage2(3, 0, SUB, 0, 4, 6, nc.vector.tensor_copy)
-        stage2(3, SUB, SUB, 0, 2, 0, nc.vector.tensor_copy)
-        stage2(3, SUB, SUB, 2, 2, 1, nc.scalar.copy)
+        h_all = keep.tile([P, PACK * J], BF16, name="h_all", tag="slot_wd", align_bytes=64)
+        h_grouped.extend(h_all[:, PACK * c * CHUNK : PACK * (c + 1) * CHUNK] for c in range(chunks))
+        gate(4)
+        gate(5)
+        hidden(0)
+        quantise(wd_codes[:], wd_scales[:], wd_grouped[:])
+        hidden(1)
+        hidden(2)
+        quantise_h(0, 0, CHUNK)
+        result(0, 0)
+        gate(6)
+        result(0, 1)
+        gate(7)
+        hidden(3)
+        hidden(4)
+        quantise_h(1, 0, CHUNK)
+        result(1, 0)
+        result(1, 1)
+        hidden(5)
+        hidden(6)
+        quantise_h(2, 0, CHUNK)
+        quantise_h(3, 0, SUB)
+        result(2, 0)
+        result(2, 1)
+        hidden(7)
+        stage2(3, 0, SUB, 0, 2, 0, nc.vector.tensor_copy)
+        quantise_h(3, SUB, SUB)
+        stage2(3, 0, SUB, 2, 2, 1, nc.scalar.copy)
+        stage2(3, SUB, SUB, 0, 2, 2, nc.vector.tensor_copy)
+        stage2(3, SUB, SUB, 2, 2, 3, nc.scalar.copy)

@@ -27,7 +27,7 @@ LIST = 16
 RUN = 4
 HEADS = 8
 BLOCKS = J // P
-EARLY = 2
+EARLY = 4
 
 
 def tile_list_relu_none_kernel(tc, xT, wgt, wg_words, wg_scales, wu, wd, offs, out):
@@ -87,7 +87,7 @@ def tile_list_relu_none_kernel(tc, xT, wgt, wg_words, wg_scales, wu, wd, offs, o
             ws_raw[:].bitcast(I32).rearrange("p a (m t) -> p a m t", t=PACK),
         )
 
-        picked = [tile("picked%d" % a, PACK * J, F32) for a in range(PASSES)]
+        picked = [keep.tile([P, PACK * J], F32, name="picked%d" % a, tag="picked%d" % a, align_bytes=64) for a in range(PASSES)]
         widths = [J, CHUNK]
         x_grouped = [[tile("x_grouped0", PACK * J, BF16)]]
         x_codes = [[], [tile("x_codes1_%d" % c, CHUNK, U32) for c in range(2)]]
@@ -138,20 +138,19 @@ def tile_list_relu_none_kernel(tc, xT, wgt, wg_words, wg_scales, wu, wd, offs, o
         def quantise_wu(a):
             quantise(wu_codes[a][:], wu_scales[a][:], wu_grouped[a][:])
 
-        wd_grouped = tile("wd_grouped", N * PACK, BF16)
         wd_codes = tile("wd_codes", N, U32)
         wd_scales = tile("wd_scales", N, U8)
 
         banks = [psum.tile([P, PACK * SUB], F32, name="bank%d" % b) for b in range(8)]
         chunks = J // CHUNK
         pieces = J // SUB
-        gates = [tile("gate%d" % s, PACK * SUB, F32) for s in range(pieces)]
-        h_grouped = []
+        gates = {s: tile("gate%d" % s, PACK * SUB, F32)[:] for s in (0, 1, 6, 7)}
+        h_grouped = [tile("h_grouped%d" % c, PACK * CHUNK, BF16) for c in range(chunks)]
         h_codes = [tile("h_codes%d" % c, CHUNK, U32) for c in range(chunks)]
         h_scales = [tile("h_scales%d" % c, CHUNK, U8) for c in range(chunks)]
 
-        def stage1(lhs_codes, lhs_scales, s, a, first, last):
-            bank = banks[s][:].rearrange("p (t j) -> p t j", t=PACK)
+        def stage1(lhs_codes, lhs_scales, slot, s, a):
+            bank = banks[slot][:].rearrange("p (t j) -> p t j", t=PACK)
             c, j0 = divmod(s * SUB, widths[a])
             for t in range(PACK):
                 nc.tensor.matmul_mx(
@@ -160,34 +159,43 @@ def tile_list_relu_none_kernel(tc, xT, wgt, wg_words, wg_scales, wu, wd, offs, o
                     lhsT_scale=lhs_scales(a, t),
                     rhs=x_codes[a][c][:, j0 : j0 + SUB].bitcast(FP8X4),
                     rhs_scale=x_scales[a][c][:, j0 : j0 + SUB],
-                    start=(first and t == 0),
-                    stop=(last and t == PACK - 1),
+                    start=(a == 0 and t == 0),
+                    stop=(a == PASSES - 1 and t == PACK - 1),
                 )
+
+        def gate_bank(s):
+            return s if s < EARLY else s % 2
+
+        def up_bank(s):
+            return EARLY + s % EARLY
 
         def gate_pass(s, a):
             stage1(
                 lambda a, t: wg_codes[:, a, 2 * P * t : 2 * P * (t + 1)].bitcast(FP4X4),
                 lambda a, t: wg_sc[:, a, P * t : P * (t + 1)],
-                s, a, a == 0, a == 1)
+                gate_bank(s), s, a)
+
+        def up_pass(s, a):
+            stage1(
+                lambda a, t: wu_codes[a][:, P * t : P * (t + 1)].bitcast(FP8X4),
+                lambda a, t: wu_scales[a][:, P * t : P * (t + 1)],
+                up_bank(s), s, a)
 
         def by_token(s):
             return banks[s][:].rearrange("p (t j) -> p j t", t=PACK)
 
         def gate(s):
-            gate_pass(s, 1)
-            nc.scalar.copy(gates[s][:].rearrange("p (j t) -> p j t", t=PACK), by_token(s))
+            for a in range(1 if s < EARLY else 0, PASSES):
+                gate_pass(s, a)
+            nc.scalar.copy(gates[s].rearrange("p (j t) -> p j t", t=PACK), by_token(gate_bank(s)))
 
         def hidden(s):
-            order = (0, 1) if s < EARLY else (1, 0)
-            for a in order:
-                stage1(
-                    lambda a, t: wu_codes[a][:, P * t : P * (t + 1)].bitcast(FP8X4),
-                    lambda a, t: wu_scales[a][:, P * t : P * (t + 1)],
-                    s, a, a == order[0], a == order[1])
+            for a in range(1 if s < EARLY else 0, PASSES):
+                up_pass(s, a)
             c, j0 = divmod(s * SUB, CHUNK)
             nc.vector.scalar_tensor_tensor(
                 h_grouped[c][:, PACK * j0 : PACK * (j0 + SUB)].rearrange("p (j t) -> p j t", t=PACK),
-                gates[s][:].rearrange("p (j t) -> p j t", t=PACK), 0.0, by_token(s), MAX, MULT)
+                gates[s].rearrange("p (j t) -> p j t", t=PACK), 0.0, by_token(up_bank(s)), MAX, MULT)
 
         def quantise_h(c, j0, width):
             quantise(h_codes[c][:, j0 : j0 + width], h_scales[c][:, j0 : j0 + width],
@@ -213,8 +221,8 @@ def tile_list_relu_none_kernel(tc, xT, wgt, wg_words, wg_scales, wu, wd, offs, o
             first = c * CHUNK + j0
             nc.sync.dma_start(out_rows[:, v0 : v0 + count, first : first + width], y[:])
 
-        def result(c, u):
-            stage2(c, 0, CHUNK, 2 * u, 2, 2 * c + u, nc.scalar.copy)
+        def result(c, u, slot, copy):
+            stage2(c, 0, CHUNK, 2 * u, 2, slot, copy)
 
         parts = [(0, CHUNK, nc.vector.tensor_copy), (J - CHUNK, CHUNK, nc.vector.tensor_copy), (CHUNK, HALF, nc.scalar.copy)]
         for bank in (banks[3], banks[4]):
@@ -251,55 +259,54 @@ def tile_list_relu_none_kernel(tc, xT, wgt, wg_words, wg_scales, wu, wd, offs, o
         for c in range(chunks):
             group_pair(c, 0)
         gather(1, 2, 0, J)
-        for s in range(pieces):
+        for s in range(EARLY):
             gate_pass(s, 0)
+        for s in range(EARLY):
+            up_pass(s, 0)
 
         for c in range(chunks):
             gather(1, 3, c * CHUNK, CHUNK)
-        group_pair(0, 2)
-        group_pair(1, 2)
-        group_pair(2, 2)
-        group_pair(3, 2)
+        for c in range(chunks):
+            group_pair(c, 2)
         quantise_x(1, 0)
         quantise_x(1, 1)
         cast_wu(nc.vector.tensor_copy, 1)
         late = keep.tile([P, 2 * CHUNK], U32, name="late_codes", tag="slot1", align_bytes=64)
         x_codes[1].extend([late[:, :CHUNK], late[:, CHUNK:]])
+        quantise_wu(1)
+        quantise_x(1, 2)
         gate(0)
         gate(1)
+        wd_grouped = wu_grouped[1]
+        interleave(nc.scalar.copy, wd_grouped[:], wd_raw[:])
+        held = keep.tile([P, 4 * PACK * SUB], F32, name="gates_held", tag="slot_wd", align_bytes=64)
+        for s in range(2, 6):
+            gates[s] = held[:, (s - 2) * PACK * SUB : (s - 1) * PACK * SUB]
+        hidden(0)
+        hidden(1)
+        quantise_x(1, 3)
+        quantise_h(0, 0, CHUNK)
+        quantise(wd_codes[:], wd_scales[:], wd_grouped[:])
         gate(2)
         gate(3)
-        quantise_x(1, 2)
-        quantise_x(1, 3)
-        quantise_wu(1)
-        interleave(nc.vector.tensor_copy, wd_grouped[:], wd_raw[:])
-        h_all = keep.tile([P, PACK * J], BF16, name="h_all", tag="slot_wd", align_bytes=64)
-        h_grouped.extend(h_all[:, PACK * c * CHUNK : PACK * (c + 1) * CHUNK] for c in range(chunks))
         gate(4)
+        result(0, 0, 2, nc.scalar.copy)
         gate(5)
-        hidden(0)
-        quantise(wd_codes[:], wd_scales[:], wd_grouped[:])
-        hidden(1)
-        hidden(2)
-        quantise_h(0, 0, CHUNK)
-        result(0, 0)
+        result(0, 1, 3, nc.scalar.copy)
         gate(6)
-        result(0, 1)
         gate(7)
+        hidden(2)
         hidden(3)
         hidden(4)
         quantise_h(1, 0, CHUNK)
-        result(1, 0)
-        result(1, 1)
         hidden(5)
+        result(1, 0, 4, nc.scalar.copy)
+        result(1, 1, 5, nc.scalar.copy)
         hidden(6)
         quantise_h(2, 0, CHUNK)
-        quantise_h(3, 0, SUB)
-        result(2, 0)
-        result(2, 1)
         hidden(7)
-        stage2(3, 0, SUB, 0, 2, 0, nc.vector.tensor_copy)
-        quantise_h(3, SUB, SUB)
-        stage2(3, 0, SUB, 2, 2, 1, nc.scalar.copy)
-        stage2(3, SUB, SUB, 0, 2, 2, nc.vector.tensor_copy)
-        stage2(3, SUB, SUB, 2, 2, 3, nc.scalar.copy)
+        result(2, 0, 2, nc.scalar.copy)
+        result(2, 1, 3, nc.scalar.copy)
+        quantise_h(3, 0, CHUNK)
+        result(3, 0, 0, nc.vector.tensor_copy)
+        result(3, 1, 1, nc.scalar.copy)

@@ -27,7 +27,8 @@ LIST = 16
 RUN = 4
 HEADS = 8
 BLOCKS = J // P
-EARLY = 4
+EARLY_GATES = 6
+EARLY_UPS = 2
 
 
 def tile_list_relu_none_kernel(tc, xT, wgt, wg_words, wg_scales, wu, wd, offs, out):
@@ -46,7 +47,7 @@ def tile_list_relu_none_kernel(tc, xT, wgt, wg_words, wg_scales, wu, wd, offs, o
             for a in range(PASSES)
         ]
         wu_raw = [keep.tile([P, PACK, R], F32, name="wu_raw%d" % a, tag="slot%d" % a, align_bytes=64) for a in range(PASSES)]
-        wd_raw = keep.tile([P, PACK, N], F32, name="wd_raw", tag="slot_wd", align_bytes=64)
+        wd_raw = [keep.tile([P, PACK, N // 2], F32, name="wd_raw%d" % u, tag="slot_wd%d" % u, align_bytes=64) for u in range(2)]
         wg_raw = keep.tile([P, PASSES, 2 * R], U8, name="wg_raw")
         ws_raw = keep.tile([P, PASSES, R], U8, name="ws_raw")
         nc.vector.memset(ws_raw[:].bitcast(I32), 0)
@@ -58,6 +59,10 @@ def tile_list_relu_none_kernel(tc, xT, wgt, wg_words, wg_scales, wu, wd, offs, o
 
         def load_x(a, i):
             nc.sync.dma_start(planes[a][i][:], x_rows[a, i])
+
+        def load_wd(u):
+            for t in range(PACK):
+                nc.sync.dma_start(wd_raw[u][:, t, :], wd_rows[t][:, :, u * N // 2 : (u + 1) * N // 2])
 
         head_rows = tile("head_rows", P, F32)
         nc.vector.memset(head_rows[HEADS * BLOCKS :, :], 0.0)
@@ -75,28 +80,29 @@ def tile_list_relu_none_kernel(tc, xT, wgt, wg_words, wg_scales, wu, wd, offs, o
         for q in range(4):
             nc.sync.dma_start(ws_raw[32 * q : 32 * q + 4].bitcast(I32), ws_rows[4 * q : 4 * q + 4].bitcast(I32))
         load_x(1, 2)
+        load_wd(0)
         load_x(1, 3)
         nc.sync.dma_start(wu_raw[1][:], wu_rows[1])
-        for t in range(PACK):
-            nc.sync.dma_start(wd_raw[:, t, :], wd_rows[t])
+        load_wd(1)
 
         wg_codes = keep.tile([P, PASSES, 2 * R], U8, name="wg_codes", align_bytes=64)
         wg_sc = keep.tile([P, PASSES, R], U8, name="wg_sc", align_bytes=64)
-        nc.vector.tensor_copy(
-            wg_sc[:].bitcast(I32).rearrange("p a (t m) -> p a m t", t=PACK),
-            ws_raw[:].bitcast(I32).rearrange("p a (m t) -> p a m t", t=PACK),
-        )
 
-        picked = [keep.tile([P, PACK * J], F32, name="picked%d" % a, tag="picked%d" % a, align_bytes=64) for a in range(PASSES)]
+        picked = [tile("picked%d" % a, PACK * J, F32) for a in range(PASSES)]
         widths = [J, CHUNK]
         x_grouped = [[tile("x_grouped0", PACK * J, BF16)]]
-        x_codes = [[], [tile("x_codes1_%d" % c, CHUNK, U32) for c in range(2)]]
+        x_codes = [[tile("x_codes0", J, U32)], [tile("x_codes1_%d" % c, CHUNK, U32) for c in range(2)]]
         x_scales = [[tile("x_scales%d_%d" % (a, c), widths[a], U8) for c in range(J // widths[a])] for a in range(PASSES)]
+
+        def picks(a, i0, j0, width):
+            if a == 0:
+                return picked[0][:].rearrange("p (i j) -> p i j", j=J)[:, :, j0 : j0 + width]
+            return picked[1][:].rearrange("p (i j) -> p i j", j=J)[:, i0 // 2 * 2 : i0 // 2 * 2 + 2, j0 : j0 + width]
 
         def gather(a, i, j0, width):
             cols = slice(j0 // LIST, (j0 + width) // LIST)
             nc.vector.tensor_tensor(
-                picked[a][:, i * J + j0 : i * J + j0 + width],
+                picks(a, i, j0, width)[:, i if a == 0 else i % 2, :],
                 planes[a][i][:].indirect(offsets[:, cols]),
                 weight[:, j0 : j0 + width],
                 MULT,
@@ -113,7 +119,7 @@ def tile_list_relu_none_kernel(tc, xT, wgt, wg_words, wg_scales, wu, wd, offs, o
             interleave(nc.scalar.copy, x_grouped[0][0][:, PACK * j0 : PACK * (j0 + width)], src)
 
         def group_pair(c, i0):
-            src = picked[1][:].rearrange("p (i j) -> p i j", i=PACK)[:, i0 : i0 + 2, c * CHUNK : (c + 1) * CHUNK]
+            src = picks(1, i0, c * CHUNK, CHUNK)
             nc.scalar.copy(
                 x_grouped[1][c].rearrange("p (c e i) -> p c i e", e=4, i=PACK)[:, :, i0 : i0 + 2, :],
                 src.rearrange("p i (c e) -> p c i e", e=4),
@@ -138,18 +144,16 @@ def tile_list_relu_none_kernel(tc, xT, wgt, wg_words, wg_scales, wu, wd, offs, o
         def quantise_wu(a):
             quantise(wu_codes[a][:], wu_scales[a][:], wu_grouped[a][:])
 
-        wd_codes = tile("wd_codes", N, U32)
-        wd_scales = tile("wd_scales", N, U8)
 
         banks = [psum.tile([P, PACK * SUB], F32, name="bank%d" % b) for b in range(8)]
         chunks = J // CHUNK
         pieces = J // SUB
-        gates = {s: tile("gate%d" % s, PACK * SUB, F32)[:] for s in (0, 1, 6, 7)}
+        gates = {s: keep.tile([P, PACK * SUB], F32, name="gate%d" % s, tag="gate%d" % s, align_bytes=64)[:] for s in (0, 1, 6, 7)}
         h_grouped = [tile("h_grouped%d" % c, PACK * CHUNK, BF16) for c in range(chunks)]
         h_codes = [tile("h_codes%d" % c, CHUNK, U32) for c in range(chunks)]
         h_scales = [tile("h_scales%d" % c, CHUNK, U8) for c in range(chunks)]
 
-        def stage1(lhs_codes, lhs_scales, slot, s, a):
+        def stage1(lhs_codes, lhs_scales, slot, s, a, opens):
             bank = banks[slot][:].rearrange("p (t j) -> p t j", t=PACK)
             c, j0 = divmod(s * SUB, widths[a])
             for t in range(PACK):
@@ -159,39 +163,46 @@ def tile_list_relu_none_kernel(tc, xT, wgt, wg_words, wg_scales, wu, wd, offs, o
                     lhsT_scale=lhs_scales(a, t),
                     rhs=x_codes[a][c][:, j0 : j0 + SUB].bitcast(FP8X4),
                     rhs_scale=x_scales[a][c][:, j0 : j0 + SUB],
-                    start=(a == 0 and t == 0),
-                    stop=(a == PASSES - 1 and t == PACK - 1),
+                    start=(opens and t == 0),
+                    stop=(not opens and t == PACK - 1),
                 )
 
         def gate_bank(s):
-            return s if s < EARLY else s % 2
+            return s if s < EARLY_GATES else s - 4
 
         def up_bank(s):
-            return EARLY + s % EARLY
+            return (EARLY_GATES if s % 4 < 2 else 0) + s % 2
 
-        def gate_pass(s, a):
+        def gate_pass(s, a, opens):
             stage1(
                 lambda a, t: wg_codes[:, a, 2 * P * t : 2 * P * (t + 1)].bitcast(FP4X4),
                 lambda a, t: wg_sc[:, a, P * t : P * (t + 1)],
-                gate_bank(s), s, a)
+                gate_bank(s), s, a, opens)
 
-        def up_pass(s, a):
+        def up_pass(s, a, opens):
             stage1(
                 lambda a, t: wu_codes[a][:, P * t : P * (t + 1)].bitcast(FP8X4),
                 lambda a, t: wu_scales[a][:, P * t : P * (t + 1)],
-                up_bank(s), s, a)
+                up_bank(s), s, a, opens)
 
         def by_token(s):
             return banks[s][:].rearrange("p (t j) -> p j t", t=PACK)
 
+        def gate_sums(s):
+            if s >= EARLY_GATES:
+                gate_pass(s, 0, True)
+            gate_pass(s, 1, False)
+
+        def up_sums(s):
+            first = 1 if s > EARLY_UPS else 0
+            if s >= EARLY_UPS:
+                up_pass(s, first, True)
+            up_pass(s, 1 - first, False)
+
         def gate(s):
-            for a in range(1 if s < EARLY else 0, PASSES):
-                gate_pass(s, a)
             nc.scalar.copy(gates[s].rearrange("p (j t) -> p j t", t=PACK), by_token(gate_bank(s)))
 
         def hidden(s):
-            for a in range(1 if s < EARLY else 0, PASSES):
-                up_pass(s, a)
             c, j0 = divmod(s * SUB, CHUNK)
             nc.vector.scalar_tensor_tensor(
                 h_grouped[c][:, PACK * j0 : PACK * (j0 + SUB)].rearrange("p (j t) -> p j t", t=PACK),
@@ -245,9 +256,11 @@ def tile_list_relu_none_kernel(tc, xT, wgt, wg_words, wg_scales, wu, wd, offs, o
             gather(0, 3, h * HALF, HALF)
             group_first(h * HALF, HALF)
         gather(1, 0, 0, J)
-        gather(1, 1, 0, J)
-        x_codes[0].append(keep.tile([P, J], U32, name="x_codes0", tag="plane11", align_bytes=64))
-        quantise_x(0, 0)
+        for h in range(2):
+            cols = slice(h * HALF, (h + 1) * HALF)
+            quantise(x_codes[0][0][:, cols], x_scales[0][0][:, cols], x_grouped[0][0][:, PACK * h * HALF : PACK * (h + 1) * HALF])
+        for h in range(2):
+            gather(1, 1, h * HALF, HALF)
         nc.vector.tensor_copy(
             wg_codes[:].bitcast(I32).rearrange("p a (t m w) -> p a m t w", t=PACK, w=2),
             wg_raw[:].bitcast(I32).rearrange("p a (m t w) -> p a m t w", t=PACK, w=2),
@@ -258,55 +271,82 @@ def tile_list_relu_none_kernel(tc, xT, wgt, wg_words, wg_scales, wu, wd, offs, o
         x_grouped.append([grouped1[:, PACK * c * CHUNK : PACK * (c + 1) * CHUNK] for c in range(chunks)])
         for c in range(chunks):
             group_pair(c, 0)
+        nc.vector.tensor_copy(
+            wg_sc[:].bitcast(I32).rearrange("p a (t m) -> p a m t", t=PACK),
+            ws_raw[:].bitcast(I32).rearrange("p a (m t) -> p a m t", t=PACK),
+        )
         gather(1, 2, 0, J)
-        for s in range(EARLY):
-            gate_pass(s, 0)
-        for s in range(EARLY):
-            up_pass(s, 0)
+        for s in range(EARLY_UPS):
+            up_pass(s, 0, True)
+        for s in range(EARLY_GATES):
+            gate_pass(s, 0, True)
+        wd_grouped = [tile("wd_grouped%d" % u, PACK * N // 2, BF16) for u in range(2)]
+        interleave(nc.scalar.copy, wd_grouped[0][:], wd_raw[0][:])
 
         for c in range(chunks):
             gather(1, 3, c * CHUNK, CHUNK)
         for c in range(chunks):
             group_pair(c, 2)
         quantise_x(1, 0)
+        gate_sums(0)
+        gate_sums(1)
         quantise_x(1, 1)
+        gate_sums(2)
+        gate_sums(3)
+        gate(0)
+        gate(1)
         cast_wu(nc.vector.tensor_copy, 1)
         late = keep.tile([P, 2 * CHUNK], U32, name="late_codes", tag="slot1", align_bytes=64)
         x_codes[1].extend([late[:, :CHUNK], late[:, CHUNK:]])
-        quantise_wu(1)
         quantise_x(1, 2)
-        gate(0)
-        gate(1)
-        wd_grouped = wu_grouped[1]
-        interleave(nc.scalar.copy, wd_grouped[:], wd_raw[:])
-        held = keep.tile([P, 4 * PACK * SUB], F32, name="gates_held", tag="slot_wd", align_bytes=64)
+        gate_sums(4)
+        gate_sums(5)
+        quantise_wu(1)
+        quantise_x(1, 3)
+        for s in range(4):
+            up_sums(s)
+        interleave(nc.scalar.copy, wd_grouped[1][:], wd_raw[1][:])
+        held = keep.tile([P, 4 * PACK * SUB], F32, name="gates_held", tag="slot_wd1", align_bytes=64)
         for s in range(2, 6):
             gates[s] = held[:, (s - 2) * PACK * SUB : (s - 1) * PACK * SUB]
         hidden(0)
         hidden(1)
-        quantise_x(1, 3)
+        wd_codes = tile("wd_codes", N, U32)
+        wd_scales = keep.tile([P, N], U8, name="wd_scales", tag="gate0", align_bytes=64)
+
+        def quantise_wd(u):
+            cols = slice(u * N // 2, (u + 1) * N // 2)
+            quantise(wd_codes[:, cols], wd_scales[:, cols], wd_grouped[u][:])
+
+        quantise_wd(0)
         quantise_h(0, 0, CHUNK)
-        quantise(wd_codes[:], wd_scales[:], wd_grouped[:])
+        quantise_wd(1)
         gate(2)
         gate(3)
         gate(4)
-        result(0, 0, 2, nc.scalar.copy)
         gate(5)
-        result(0, 1, 3, nc.scalar.copy)
+        up_sums(4)
+        gate_sums(6)
+        result(0, 0, 4, nc.scalar.copy)
+        up_sums(5)
+        gate_sums(7)
         gate(6)
-        gate(7)
+        result(0, 1, 5, nc.scalar.copy)
         hidden(2)
+        up_sums(6)
         hidden(3)
+        gate(7)
         hidden(4)
         quantise_h(1, 0, CHUNK)
+        result(1, 0, 2, nc.scalar.copy)
+        up_sums(7)
+        result(1, 1, 3, nc.scalar.copy)
         hidden(5)
-        result(1, 0, 4, nc.scalar.copy)
-        result(1, 1, 5, nc.scalar.copy)
         hidden(6)
         quantise_h(2, 0, CHUNK)
         hidden(7)
-        result(2, 0, 2, nc.scalar.copy)
-        result(2, 1, 3, nc.scalar.copy)
+        result(2, 0, 6, nc.scalar.copy)
+        result(2, 1, 7, nc.scalar.copy)
         quantise_h(3, 0, CHUNK)
-        result(3, 0, 0, nc.vector.tensor_copy)
-        result(3, 1, 1, nc.scalar.copy)
+        result(3, 0, 4, nc.vector.tensor_copy)
+        result(3, 1, 5, nc.scalar.copy)

@@ -35,10 +35,14 @@ def tile_list_relu_none_kernel(tc, xT, wgt, wg_words, wg_scales, wu, wd, offs, o
     nc = tc.nc
     with ExitStack() as ctx:
         keep = ctx.enter_context(tc.tile_pool(name="keep", bufs=1))
+        shared = ctx.enter_context(tc.tile_pool(name="shared", bufs=1))
         psum = ctx.enter_context(tc.psum_pool(name="psum", bufs=1))
 
         def tile(name, width, dtype):
             return keep.tile([P, width], dtype, name=name, align_bytes=64)
+
+        def tile_at(name, shape, dtype, offset):
+            return shared.tile([P] + shape, dtype, name=name, offset=offset, align_bytes=64)
 
         offsets = keep.tile([P, J // LIST], U16, name="offsets")
         weight = tile("weight", J, F32)
@@ -46,11 +50,12 @@ def tile_list_relu_none_kernel(tc, xT, wgt, wg_words, wg_scales, wu, wd, offs, o
             [keep.tile([P, T], F32, name="x%d%d" % (a, i), tag="plane%d%d" % (a, i), align_bytes=64) for i in range(PACK)]
             for a in range(PASSES)
         ]
-        wu_raw = [keep.tile([P, PACK, R], F32, name="wu_raw%d" % a, tag="slot%d" % a, align_bytes=64) for a in range(PASSES)]
-        wd_raw = [keep.tile([P, PACK, N // 2], F32, name="wd_raw%d" % u, tag="slot_wd%d" % u, align_bytes=64) for u in range(2)]
+        late_rows = tile("late_rows", 2 * J + PACK * R, F32)
+        wu_raw = [tile("wu_raw0", PACK * R, F32)[:], late_rows[:, 2 * J :]]
+        wu_raw = [raw.rearrange("p (i r) -> p i r", i=PACK) for raw in wu_raw]
+        wd_raw = [tile_at("wd_raw0", [PACK, N // 2], F32, 1024), keep.tile([P, PACK, N // 2], F32, name="wd_raw1", tag="slot_wd1", align_bytes=64)]
         wg_raw = keep.tile([P, PASSES, 2 * R], U8, name="wg_raw")
         ws_raw = keep.tile([P, PASSES, R], U8, name="ws_raw")
-        nc.vector.memset(ws_raw[:].bitcast(I32), 0)
 
         x_rows = xT.rearrange("(a p i) t -> a i p t", a=PASSES, i=PACK)
         wu_rows = wu.rearrange("(a p i) r -> a p i r", a=PASSES, i=PACK)
@@ -67,42 +72,40 @@ def tile_list_relu_none_kernel(tc, xT, wgt, wg_words, wg_scales, wu, wd, offs, o
         head_rows = tile("head_rows", P, F32)
         nc.vector.memset(head_rows[HEADS * BLOCKS :, :], 0.0)
         nc.scalar.dma_start(head_rows[: HEADS * BLOCKS, :], wgt.rearrange("(g r) (b c) -> r g b c", r=LIST, c=P)[0])
-        identity = tile("identity", P, F32)
+        for q in range(4):
+            nc.scalar.dma_start(ws_raw[32 * q : 32 * q + 4].bitcast(I32), ws_rows[4 * q : 4 * q + 4].bitcast(I32))
+        identity = keep.tile([P, P], F32, name="identity", tag="identity", align_bytes=64)
         make_identity(nc, identity[:])
         nc.sync.dma_start(offsets[:], offs)
         load_x(0, 0)
         for i in range(1, PACK):
             load_x(0, i)
         load_x(1, 0)
-        load_x(1, 1)
-        nc.sync.dma_start(wu_raw[0][:], wu_rows[0])
+        nc.sync.dma_start(wu_raw[0], wu_rows[0])
         nc.sync.dma_start(wg_raw[:].bitcast(I32), wg_words.rearrange("a p b -> p a b").bitcast(I32))
-        for q in range(4):
-            nc.sync.dma_start(ws_raw[32 * q : 32 * q + 4].bitcast(I32), ws_rows[4 * q : 4 * q + 4].bitcast(I32))
-        load_x(1, 2)
+        load_x(1, 1)
         load_wd(0)
+        load_x(1, 2)
         load_x(1, 3)
-        nc.sync.dma_start(wu_raw[1][:], wu_rows[1])
+        nc.sync.dma_start(wu_raw[1], wu_rows[1])
         load_wd(1)
 
-        wg_codes = keep.tile([P, PASSES, 2 * R], U8, name="wg_codes", align_bytes=64)
-        wg_sc = keep.tile([P, PASSES, R], U8, name="wg_sc", align_bytes=64)
-
-        picked = [tile("picked%d" % a, PACK * J, F32) for a in range(PASSES)]
+        picked = [keep.tile([P, 2, J], F32, name="picked%d" % u, align_bytes=64) for u in range(2 * PASSES - 1)]
+        picked.append(late_rows[:, : 2 * J].rearrange("p (i j) -> p i j", i=2))
         widths = [J, CHUNK]
-        x_grouped = [[tile("x_grouped0", PACK * J, BF16)]]
+        x_grouped = [tile("x_grouped0", PACK * J, BF16)]
         x_codes = [[tile("x_codes0", J, U32)], [tile("x_codes1_%d" % c, CHUNK, U32) for c in range(2)]]
         x_scales = [[tile("x_scales%d_%d" % (a, c), widths[a], U8) for c in range(J // widths[a])] for a in range(PASSES)]
 
-        def picks(a, i0, j0, width):
-            if a == 0:
-                return picked[0][:].rearrange("p (i j) -> p i j", j=J)[:, :, j0 : j0 + width]
-            return picked[1][:].rearrange("p (i j) -> p i j", j=J)[:, i0 // 2 * 2 : i0 // 2 * 2 + 2, j0 : j0 + width]
+        def picks(a, i, j0, width):
+            if (a, i // 2, j0) == (1, 1, J - CHUNK):
+                return late_rows[:].rearrange("p (i j) -> p i j", i=2)[:, :, :CHUNK]
+            return picked[2 * a + i // 2][:, :, j0 : j0 + width]
 
         def gather(a, i, j0, width):
             cols = slice(j0 // LIST, (j0 + width) // LIST)
             nc.vector.tensor_tensor(
-                picks(a, i, j0, width)[:, i if a == 0 else i % 2, :],
+                picks(a, i, j0, width)[:, i % 2, :],
                 planes[a][i][:].indirect(offsets[:, cols]),
                 weight[:, j0 : j0 + width],
                 MULT,
@@ -114,41 +117,39 @@ def tile_list_relu_none_kernel(tc, xT, wgt, wg_words, wg_scales, wu, wd, offs, o
                 src.rearrange("p i (c e) -> p c i e", e=4),
             )
 
-        def group_first(j0, width):
-            src = picked[0][:].rearrange("p (i j) -> p i j", i=PACK)[:, :, j0 : j0 + width]
-            interleave(nc.scalar.copy, x_grouped[0][0][:, PACK * j0 : PACK * (j0 + width)], src)
-
-        def group_pair(c, i0):
-            src = picks(1, i0, c * CHUNK, CHUNK)
+        def group_pair(a, i0, j0, width):
+            words = x_grouped[a][:, PACK * j0 : PACK * (j0 + width)]
             nc.scalar.copy(
-                x_grouped[1][c].rearrange("p (c e i) -> p c i e", e=4, i=PACK)[:, :, i0 : i0 + 2, :],
-                src.rearrange("p i (c e) -> p c i e", e=4),
+                words.rearrange("p (c e i) -> p c i e", e=4, i=PACK)[:, :, i0 : i0 + 2, :],
+                picks(a, i0, j0, width).rearrange("p i (c e) -> p c i e", e=4),
             )
 
         def quantise(codes, scales, grouped):
             nc.vector.quantize_mx(out=codes.bitcast(FP8X4), scales=scales, in_=grouped)
 
         def quantise_x(a, c):
-            quantise(x_codes[a][c][:, :], x_scales[a][c][:], x_grouped[a][c][:, :])
+            quantise(x_codes[a][c][:, :], x_scales[a][c][:], x_grouped[a][:, PACK * c * widths[a] : PACK * (c + 1) * widths[a]])
 
-        wu_grouped = [tile("wu_grouped%d" % a, R * PACK, BF16) for a in range(PASSES)]
-        wu_codes = [tile("wu_codes%d" % a, R, U32) for a in range(PASSES)]
+        wu_grouped = [keep.tile([P, R * PACK], BF16, name="wu_grouped%d" % a, tag="wu_grouped%d" % a, align_bytes=64) for a in range(PASSES)]
+        wu_codes = {(0, 0): tile("wu_codes00", R // 2, U32)[:]}
+        second_codes = tile("wu_codes1", R, U32)
+        wu_codes[1, 0], wu_codes[1, 1] = second_codes[:, : R // 2], second_codes[:, R // 2 :]
         wu_scales = [tile("wu_scales%d" % a, R, U8) for a in range(PASSES)]
 
-        def cast_wu(engine_copy, a):
+        def cast_wu(engine_copy, a, t0, count):
             engine_copy(
-                wu_grouped[a][:].rearrange("p (t m e i) -> p m t i e", t=PACK, e=RUN, i=PACK),
-                wu_raw[a][:].rearrange("p i (m t e) -> p m t i e", t=PACK, e=RUN),
+                wu_grouped[a][:].rearrange("p (t m e i) -> p m t i e", t=PACK, e=RUN, i=PACK)[:, :, t0 : t0 + count],
+                wu_raw[a].rearrange("p i (m t e) -> p m t i e", t=PACK, e=RUN)[:, :, t0 : t0 + count],
             )
 
-        def quantise_wu(a):
-            quantise(wu_codes[a][:], wu_scales[a][:], wu_grouped[a][:])
+        def quantise_wu(a, u):
+            quantise(wu_codes[a, u], wu_scales[a][:, u * R // 2 : (u + 1) * R // 2], wu_grouped[a][:, u * 2 * R : (u + 1) * 2 * R])
 
 
         banks = [psum.tile([P, PACK * SUB], F32, name="bank%d" % b) for b in range(8)]
         chunks = J // CHUNK
         pieces = J // SUB
-        gates = {s: keep.tile([P, PACK * SUB], F32, name="gate%d" % s, tag="gate%d" % s, align_bytes=64)[:] for s in (0, 1, 6, 7)}
+        gates = {s: keep.tile([P, PACK * SUB], F32, name="gate%d" % s, tag="gate%d" % s, align_bytes=64)[:] for s in range(pieces)}
         h_grouped = [tile("h_grouped%d" % c, PACK * CHUNK, BF16) for c in range(chunks)]
         h_codes = [tile("h_codes%d" % c, CHUNK, U32) for c in range(chunks)]
         h_scales = [tile("h_scales%d" % c, CHUNK, U8) for c in range(chunks)]
@@ -181,7 +182,7 @@ def tile_list_relu_none_kernel(tc, xT, wgt, wg_words, wg_scales, wu, wd, offs, o
 
         def up_pass(s, a, opens):
             stage1(
-                lambda a, t: wu_codes[a][:, P * t : P * (t + 1)].bitcast(FP8X4),
+                lambda a, t: wu_codes[a, t // 2][:, P * (t % 2) : P * (t % 2 + 1)].bitcast(FP8X4),
                 lambda a, t: wu_scales[a][:, P * t : P * (t + 1)],
                 up_bank(s), s, a, opens)
 
@@ -190,14 +191,13 @@ def tile_list_relu_none_kernel(tc, xT, wgt, wg_words, wg_scales, wu, wd, offs, o
 
         def gate_sums(s):
             if s >= EARLY_GATES:
-                gate_pass(s, 0, True)
-            gate_pass(s, 1, False)
+                gate_pass(s, 1, True)
+            gate_pass(s, int(s < EARLY_GATES), False)
 
         def up_sums(s):
-            first = 1 if s > EARLY_UPS else 0
-            if s >= EARLY_UPS:
-                up_pass(s, first, True)
-            up_pass(s, 1 - first, False)
+            if s >= 4:
+                up_pass(s, 0, True)
+            up_pass(s, 1, False)
 
         def gate(s):
             nc.scalar.copy(gates[s].rearrange("p (j t) -> p j t", t=PACK), by_token(gate_bank(s)))
@@ -250,65 +250,72 @@ def tile_list_relu_none_kernel(tc, xT, wgt, wg_words, wg_scales, wu, wd, offs, o
             copy(weight[:, j0 : j0 + width], banks[n][:, :width])
         for j0, width, copy in parts:
             gather(0, 0, j0, width)
+        wg_sc = keep.tile([P, PASSES, R], U8, name="wg_sc", tag="identity", align_bytes=64)
+        nc.gpsimd.memset(wg_sc[:].bitcast(U32), 0)
+        for q in range(4):
+            nc.scalar.copy(
+                wg_sc[32 * q : 32 * q + 4].bitcast(U32).rearrange("p a (t m) -> p a m t", t=PACK),
+                ws_raw[32 * q : 32 * q + 4].bitcast(U32).rearrange("p a (m t) -> p a m t", t=PACK),
+            )
         gather(0, 1, 0, J)
+        group_pair(0, 0, 0, J)
         gather(0, 2, 0, J)
         for h in range(2):
             gather(0, 3, h * HALF, HALF)
-            group_first(h * HALF, HALF)
+            group_pair(0, 2, h * HALF, HALF)
         gather(1, 0, 0, J)
-        for h in range(2):
-            cols = slice(h * HALF, (h + 1) * HALF)
-            quantise(x_codes[0][0][:, cols], x_scales[0][0][:, cols], x_grouped[0][0][:, PACK * h * HALF : PACK * (h + 1) * HALF])
+        quantise_x(0, 0)
+        cast_wu(nc.scalar.copy, 0, 0, 2)
+        quantise_wu(0, 0)
+        cast_wu(nc.scalar.copy, 0, 2, 2)
         for h in range(2):
             gather(1, 1, h * HALF, HALF)
-        nc.vector.tensor_copy(
-            wg_codes[:].bitcast(I32).rearrange("p a (t m w) -> p a m t w", t=PACK, w=2),
-            wg_raw[:].bitcast(I32).rearrange("p a (m t w) -> p a m t w", t=PACK, w=2),
+        wd_grouped = [tile("wd_grouped%d" % u, PACK * N // 2, BF16) for u in range(2)]
+        interleave(nc.scalar.copy, wd_grouped[0][:], wd_raw[0][:])
+        wg_codes = tile_at("wg_codes", [PASSES, 2 * R], U8, 0)
+        wu_codes[0, 1] = tile_at("wu_codes01", [R // 2], U32, 2048)[:]
+        x_grouped.append(tile_at("x_grouped1", [PACK * J], BF16, 3072))
+        quantise_wu(0, 1)
+        group_pair(1, 0, 0, HALF)
+        nc.scalar.copy(
+            wg_codes[:].bitcast(U32).rearrange("p a (t m w) -> p a m t w", t=PACK, w=2),
+            wg_raw[:].bitcast(U32).rearrange("p a (m t w) -> p a m t w", t=PACK, w=2),
         )
-        cast_wu(nc.scalar.copy, 0)
-        quantise_wu(0)
-        grouped1 = keep.tile([P, PACK * J], BF16, name="x_grouped1", tag="slot0", align_bytes=64)
-        x_grouped.append([grouped1[:, PACK * c * CHUNK : PACK * (c + 1) * CHUNK] for c in range(chunks)])
-        for c in range(chunks):
-            group_pair(c, 0)
-        nc.vector.tensor_copy(
-            wg_sc[:].bitcast(I32).rearrange("p a (t m) -> p a m t", t=PACK),
-            ws_raw[:].bitcast(I32).rearrange("p a (m t) -> p a m t", t=PACK),
-        )
-        gather(1, 2, 0, J)
+        group_pair(1, 0, HALF, HALF)
+        gather(1, 2, 0, J - CHUNK)
         for s in range(EARLY_UPS):
             up_pass(s, 0, True)
         for s in range(EARLY_GATES):
             gate_pass(s, 0, True)
-        wd_grouped = [tile("wd_grouped%d" % u, PACK * N // 2, BF16) for u in range(2)]
-        interleave(nc.scalar.copy, wd_grouped[0][:], wd_raw[0][:])
 
-        for c in range(chunks):
+        for c in range(chunks - 1):
             gather(1, 3, c * CHUNK, CHUNK)
-        for c in range(chunks):
-            group_pair(c, 2)
+            group_pair(1, 2, c * CHUNK, CHUNK)
         quantise_x(1, 0)
         gate_sums(0)
         gate_sums(1)
+        gather(1, 2, J - CHUNK, CHUNK)
         quantise_x(1, 1)
         gate_sums(2)
         gate_sums(3)
-        gate(0)
-        gate(1)
-        cast_wu(nc.vector.tensor_copy, 1)
-        late = keep.tile([P, 2 * CHUNK], U32, name="late_codes", tag="slot1", align_bytes=64)
-        x_codes[1].extend([late[:, :CHUNK], late[:, CHUNK:]])
+        for s in range(4):
+            gate(s)
+        for s in range(EARLY_UPS, 4):
+            up_pass(s, 0, True)
+        for t0 in (0, 2):
+            cast_wu(nc.vector.tensor_copy, 1, t0, 2)
+        for u in range(2):
+            quantise_wu(1, u)
+        for s in range(4):
+            up_sums(s)
+        gather(1, 3, J - CHUNK, CHUNK)
+        x_codes[1].append(keep.tile([P, CHUNK], U32, name="x_codes1_2", tag="wu_grouped1", align_bytes=64))
+        x_codes[1].append(tile("x_codes1_3", CHUNK, U32))
         quantise_x(1, 2)
         gate_sums(4)
         gate_sums(5)
-        quantise_wu(1)
-        quantise_x(1, 3)
-        for s in range(4):
-            up_sums(s)
-        interleave(nc.scalar.copy, wd_grouped[1][:], wd_raw[1][:])
-        held = keep.tile([P, 4 * PACK * SUB], F32, name="gates_held", tag="slot_wd1", align_bytes=64)
-        for s in range(2, 6):
-            gates[s] = held[:, (s - 2) * PACK * SUB : (s - 1) * PACK * SUB]
+        group_pair(1, 2, J - CHUNK, CHUNK)
+        interleave(nc.scalar.copy, wd_grouped[1][:, PACK * P :], wd_raw[1][:, :, P:])
         hidden(0)
         hidden(1)
         wd_codes = tile("wd_codes", N, U32)
@@ -320,33 +327,49 @@ def tile_list_relu_none_kernel(tc, xT, wgt, wg_words, wg_scales, wu, wd, offs, o
 
         quantise_wd(0)
         quantise_h(0, 0, CHUNK)
-        quantise_wd(1)
-        gate(2)
-        gate(3)
+        quantise_x(1, 3)
+        interleave(nc.vector.tensor_copy, wd_grouped[1][:, : PACK * P], wd_raw[1][:, :, :P])
         gate(4)
         gate(5)
         up_sums(4)
-        gate_sums(6)
-        result(0, 0, 4, nc.scalar.copy)
         up_sums(5)
+        result(0, 0, 4, nc.scalar.copy)
+        gate_sums(6)
         gate_sums(7)
         gate(6)
-        result(0, 1, 5, nc.scalar.copy)
+        gate(7)
         hidden(2)
+        quantise_wd(1)
+        result(0, 1, 5, nc.scalar.copy)
         up_sums(6)
         hidden(3)
-        gate(7)
         hidden(4)
         quantise_h(1, 0, CHUNK)
-        result(1, 0, 2, nc.scalar.copy)
+        result(1, 0, 4, nc.scalar.copy)
+        result(1, 1, 5, nc.scalar.copy)
         up_sums(7)
-        result(1, 1, 3, nc.scalar.copy)
         hidden(5)
-        hidden(6)
-        quantise_h(2, 0, CHUNK)
-        hidden(7)
+        quantise_h(2, 0, SUB)
+        quantise_h(2, SUB, SUB)
         result(2, 0, 6, nc.scalar.copy)
         result(2, 1, 7, nc.scalar.copy)
-        quantise_h(3, 0, CHUNK)
-        result(3, 0, 4, nc.vector.tensor_copy)
-        result(3, 1, 5, nc.scalar.copy)
+        hidden(6)
+        hidden(7)
+        last_banks = (2, 3, 4, 5)
+        for j0 in (0, SUB):
+            quantise_h(3, j0, SUB)
+            for v, slot in enumerate(last_banks):
+                nc.tensor.matmul_mx(
+                    out=banks[slot][:, j0 : j0 + SUB],
+                    lhsT=wd_codes[:, v * P : (v + 1) * P].bitcast(FP8X4),
+                    lhsT_scale=wd_scales[:, v * P : (v + 1) * P],
+                    rhs=h_codes[3][:, j0 : j0 + SUB].bitcast(FP8X4),
+                    rhs_scale=h_scales[3][:, j0 : j0 + SUB],
+                    start=True,
+                    stop=True,
+                )
+        for u in range(2):
+            y = keep.tile([P, 2, CHUNK], F32, name="y_last%d" % u)
+            nc.scalar.copy(y[:, 0, :], banks[last_banks[2 * u]][:, :CHUNK])
+            nc.vector.tensor_copy(y[:, 1, :], banks[last_banks[2 * u + 1]][:, :CHUNK])
+            nc.sync.dma_start(out_rows[:, 2 * u : 2 * u + 2, J - CHUNK :], y[:])

from contextlib import ExitStack

import concourse.mybir as mybir
from concourse.masks import make_identity

K, R, N, T, J = 1024, 512, 512, 2048, 1024
FLOPS = 2 * J * (2 * K * R + R * N)

F32 = mybir.dt.float32
BF16 = mybir.dt.bfloat16
I32 = mybir.dt.int32
U32 = mybir.dt.uint32
U16 = mybir.dt.uint16
U8 = mybir.dt.uint8
FP8X4 = mybir.dt.float8_e4m3fn_x4
FP4X4 = mybir.dt.float4_e2m1fn_x4
MULT = mybir.AluOpType.mult
MAX = mybir.AluOpType.max

P = 128
PACK = 4
PASSES = K // (P * PACK)
HALF = J // 2
CHUNK = 256
SUB = 128
LIST = 16
RUN = 4
HEADS = 8
BLOCKS = J // P
EARLY_GATES = 6
EARLY_UPS = 2


def tile_list_relu_none_kernel(tc, xT, wgt, wg_words, wg_scales, wu, wd, offs, out):
    nc = tc.nc
    with ExitStack() as ctx:
        keep = ctx.enter_context(tc.tile_pool(name="keep", bufs=1))
        shared = ctx.enter_context(tc.tile_pool(name="shared", bufs=1))
        psum = ctx.enter_context(tc.psum_pool(name="psum", bufs=1))

        def tile(name, width, dtype):
            return keep.tile([P, width], dtype, name=name, align_bytes=64)

        def tile_at(name, shape, dtype, offset):
            return shared.tile([P] + shape, dtype, name=name, offset=offset, align_bytes=64)

        offsets = keep.tile([P, J // LIST], U16, name="offsets")
        weight = tile("weight", J, F32)
        planes = [
            [keep.tile([P, T], F32, name="x%d%d" % (a, i), tag="plane%d%d" % (a, i), align_bytes=64) for i in range(PACK)]
            for a in range(PASSES)
        ]
        late_rows = tile("late_rows", 2 * J + PACK * R, F32)
        wu_raw = [tile("wu_raw0", PACK * R, F32)[:], late_rows[:, 2 * J :]]
        wu_raw = [raw.rearrange("p (i r) -> p i r", i=PACK) for raw in wu_raw]
        wd_raw = [tile_at("wd_raw0", [PACK, N // 2], F32, 1024), keep.tile([P, PACK, N // 2], F32, name="wd_raw1", tag="slot_wd1", align_bytes=64)]
        wg_raw = keep.tile([P, PASSES, 2 * R], U8, name="wg_raw")
        ws_raw = keep.tile([P, PASSES, R], U8, name="ws_raw")

        x_rows = xT.rearrange("(a p i) t -> a i p t", a=PASSES, i=PACK)
        wu_rows = wu.rearrange("(a p i) r -> a p i r", a=PASSES, i=PACK)
        wd_rows = wd.rearrange("(m t e) n -> t m e n", t=PACK, e=RUN)
        ws_rows = wg_scales.rearrange("a q r -> q a r")

        def load_x(a, i):
            nc.sync.dma_start(planes[a][i][:], x_rows[a, i])

        def load_wd(u):
            for t in range(PACK):
                nc.sync.dma_start(wd_raw[u][:, t, :], wd_rows[t][:, :, u * N // 2 : (u + 1) * N // 2])

        head_rows = tile("head_rows", P, F32)
        nc.vector.memset(head_rows[HEADS * BLOCKS :, :], 0.0)
        nc.scalar.dma_start(head_rows[: HEADS * BLOCKS, :], wgt.rearrange("(g r) (b c) -> r g b c", r=LIST, c=P)[0])
        for q in range(4):
            nc.scalar.dma_start(ws_raw[32 * q : 32 * q + 4].bitcast(I32), ws_rows[4 * q : 4 * q + 4].bitcast(I32))
        identity = keep.tile([P, P], F32, name="identity", tag="identity", align_bytes=64)
        make_identity(nc, identity[:])
        nc.sync.dma_start(offsets[:], offs)
        load_x(0, 0)
        for i in range(1, PACK):
            load_x(0, i)
        load_x(1, 0)
        nc.sync.dma_start(wu_raw[0], wu_rows[0])
        nc.sync.dma_start(wg_raw[:].bitcast(I32), wg_words.rearrange("a p b -> p a b").bitcast(I32))
        load_x(1, 1)
        load_wd(0)
        load_x(1, 2)
        load_x(1, 3)
        nc.sync.dma_start(wu_raw[1], wu_rows[1])
        load_wd(1)

        picked = [keep.tile([P, 2, J], F32, name="picked%d" % u, align_bytes=64) for u in range(2 * PASSES - 1)]
        picked.append(late_rows[:, : 2 * J].rearrange("p (i j) -> p i j", i=2))
        widths = [J, CHUNK]
        x_grouped = [tile("x_grouped0", PACK * J, BF16)]
        x_codes = [[tile("x_codes0", J, U32)], [tile("x_codes1_%d" % c, CHUNK, U32) for c in range(2)]]
        x_scales = [[tile("x_scales%d_%d" % (a, c), widths[a], U8) for c in range(J // widths[a])] for a in range(PASSES)]

        def picks(a, i, j0, width):
            if (a, i // 2, j0) == (1, 1, J - CHUNK):
                return late_rows[:].rearrange("p (i j) -> p i j", i=2)[:, :, :CHUNK]
            return picked[2 * a + i // 2][:, :, j0 : j0 + width]

        def gather(a, i, j0, width):
            cols = slice(j0 // LIST, (j0 + width) // LIST)
            nc.vector.tensor_tensor(
                picks(a, i, j0, width)[:, i % 2, :],
                planes[a][i][:].indirect(offsets[:, cols]),
                weight[:, j0 : j0 + width],
                MULT,
            )

        def interleave(engine_copy, grouped, src):
            engine_copy(
                grouped.rearrange("p (c e i) -> p c i e", e=4, i=PACK),
                src.rearrange("p i (c e) -> p c i e", e=4),
            )

        def group_pair(a, i0, j0, width):
            words = x_grouped[a][:, PACK * j0 : PACK * (j0 + width)]
            nc.scalar.copy(
                words.rearrange("p (c e i) -> p c i e", e=4, i=PACK)[:, :, i0 : i0 + 2, :],
                picks(a, i0, j0, width).rearrange("p i (c e) -> p c i e", e=4),
            )

        def quantise(codes, scales, grouped):
            nc.vector.quantize_mx(out=codes.bitcast(FP8X4), scales=scales, in_=grouped)

        def quantise_x(a, c):
            quantise(x_codes[a][c][:, :], x_scales[a][c][:], x_grouped[a][:, PACK * c * widths[a] : PACK * (c + 1) * widths[a]])

        wu_grouped = [keep.tile([P, R * PACK], BF16, name="wu_grouped%d" % a, tag="wu_grouped%d" % a, align_bytes=64) for a in range(PASSES)]
        wu_codes = {(0, 0): tile("wu_codes00", R // 2, U32)[:]}
        second_codes = tile("wu_codes1", R, U32)
        wu_codes[1, 0], wu_codes[1, 1] = second_codes[:, : R // 2], second_codes[:, R // 2 :]
        wu_scales = [tile("wu_scales%d" % a, R, U8) for a in range(PASSES)]

        def cast_wu(engine_copy, a, t0, count):
            engine_copy(
                wu_grouped[a][:].rearrange("p (t m e i) -> p m t i e", t=PACK, e=RUN, i=PACK)[:, :, t0 : t0 + count],
                wu_raw[a].rearrange("p i (m t e) -> p m t i e", t=PACK, e=RUN)[:, :, t0 : t0 + count],
            )

        def quantise_wu(a, u):
            quantise(wu_codes[a, u], wu_scales[a][:, u * R // 2 : (u + 1) * R // 2], wu_grouped[a][:, u * 2 * R : (u + 1) * 2 * R])


        banks = [psum.tile([P, PACK * SUB], F32, name="bank%d" % b) for b in range(8)]
        chunks = J // CHUNK
        pieces = J // SUB
        gates = {s: keep.tile([P, PACK * SUB], F32, name="gate%d" % s, tag="gate%d" % s, align_bytes=64)[:] for s in range(pieces)}
        h_grouped = [tile("h_grouped%d" % c, PACK * CHUNK, BF16) for c in range(chunks)]
        h_codes = [tile("h_codes%d" % c, CHUNK, U32) for c in range(chunks)]
        h_scales = [tile("h_scales%d" % c, CHUNK, U8) for c in range(chunks)]

        def stage1(lhs_codes, lhs_scales, slot, s, a, opens):
            bank = banks[slot][:].rearrange("p (t j) -> p t j", t=PACK)
            c, j0 = divmod(s * SUB, widths[a])
            for t in range(PACK):
                nc.tensor.matmul_mx(
                    out=bank[:, t, :],
                    lhsT=lhs_codes(a, t),
                    lhsT_scale=lhs_scales(a, t),
                    rhs=x_codes[a][c][:, j0 : j0 + SUB].bitcast(FP8X4),
                    rhs_scale=x_scales[a][c][:, j0 : j0 + SUB],
                    start=(opens and t == 0),
                    stop=(not opens and t == PACK - 1),
                )

        def gate_bank(s):
            return s if s < EARLY_GATES else s - 4

        def up_bank(s):
            return (EARLY_GATES if s % 4 < 2 else 0) + s % 2

        def gate_pass(s, a, opens):
            stage1(
                lambda a, t: wg_codes[:, a, 2 * P * t : 2 * P * (t + 1)].bitcast(FP4X4),
                lambda a, t: wg_sc[:, a, P * t : P * (t + 1)],
                gate_bank(s), s, a, opens)

        def up_pass(s, a, opens):
            stage1(
                lambda a, t: wu_codes[a, t // 2][:, P * (t % 2) : P * (t % 2 + 1)].bitcast(FP8X4),
                lambda a, t: wu_scales[a][:, P * t : P * (t + 1)],
                up_bank(s), s, a, opens)

        def by_token(s):
            return banks[s][:].rearrange("p (t j) -> p j t", t=PACK)

        def gate_sums(s):
            if s >= EARLY_GATES:
                gate_pass(s, 1, True)
            gate_pass(s, int(s < EARLY_GATES), False)

        def up_sums(s):
            if s >= 4:
                up_pass(s, 0, True)
            up_pass(s, 1, False)

        def gate(s):
            nc.scalar.copy(gates[s].rearrange("p (j t) -> p j t", t=PACK), by_token(gate_bank(s)))

        def hidden(s):
            c, j0 = divmod(s * SUB, CHUNK)
            nc.vector.scalar_tensor_tensor(
                h_grouped[c][:, PACK * j0 : PACK * (j0 + SUB)].rearrange("p (j t) -> p j t", t=PACK),
                gates[s].rearrange("p (j t) -> p j t", t=PACK), 0.0, by_token(up_bank(s)), MAX, MULT)

        def quantise_h(c, j0, width):
            quantise(h_codes[c][:, j0 : j0 + width], h_scales[c][:, j0 : j0 + width],
                     h_grouped[c][:, PACK * j0 : PACK * (j0 + width)])

        out_rows = out.rearrange("(v p) j -> p v j", p=P)

        def stage2(c, j0, width, v0, count, slot, copy):
            bank = banks[slot][:, : count * width].rearrange("p (v j) -> p v j", v=count)
            for v in range(count):
                n0 = (v0 + v) * P
                nc.tensor.matmul_mx(
                    out=bank[:, v, :],
                    lhsT=wd_codes[:, n0 : n0 + P].bitcast(FP8X4),
                    lhsT_scale=wd_scales[:, n0 : n0 + P],
                    rhs=h_codes[c][:, j0 : j0 + width].bitcast(FP8X4),
                    rhs_scale=h_scales[c][:, j0 : j0 + width],
                    start=True,
                    stop=True,
                )
            y = keep.tile([P, count, width], F32, name="y%d_%d_%d" % (c, j0, v0))
            copy(y[:], bank)
            first = c * CHUNK + j0
            nc.sync.dma_start(out_rows[:, v0 : v0 + count, first : first + width], y[:])

        def result(c, u, slot, copy):
            stage2(c, 0, CHUNK, 2 * u, 2, slot, copy)

        parts = [(0, CHUNK, nc.vector.tensor_copy), (J - CHUNK, CHUNK, nc.vector.tensor_copy), (CHUNK, HALF, nc.scalar.copy)]
        for bank in (banks[3], banks[4]):
            nc.tensor.transpose(bank[:, :P], head_rows[:], identity[:])
        for n, (j0, width, copy) in enumerate(parts):
            b0, count = j0 // P, width // P
            by_block = banks[3 + n // 2][:, : HEADS * BLOCKS].rearrange("p (g b) -> p b g", b=BLOCKS)
            spread = keep.tile([P, count, HEADS, LIST], F32, name="spread%d" % n)
            copy(spread[:], by_block[:, b0 : b0 + count, :].unsqueeze(3).to_broadcast([P, count, HEADS, LIST]))
            for b in range(count):
                nc.tensor.transpose(banks[n][:, P * b : P * (b + 1)], spread[:, b].rearrange("p g r -> p (g r)"), identity[:])
        for n, (j0, width, copy) in enumerate(parts):
            copy = nc.vector.tensor_copy if n == 0 else nc.scalar.copy
            copy(weight[:, j0 : j0 + width], banks[n][:, :width])
        for j0, width, copy in parts:
            gather(0, 0, j0, width)
        wg_sc = keep.tile([P, PASSES, R], U8, name="wg_sc", tag="identity", align_bytes=64)
        nc.gpsimd.memset(wg_sc[:].bitcast(U32), 0)
        for q in range(4):
            nc.scalar.copy(
                wg_sc[32 * q : 32 * q + 4].bitcast(U32).rearrange("p a (t m) -> p a m t", t=PACK),
                ws_raw[32 * q : 32 * q + 4].bitcast(U32).rearrange("p a (m t) -> p a m t", t=PACK),
            )
        gather(0, 1, 0, J)
        group_pair(0, 0, 0, J)
        gather(0, 2, 0, J)
        for h in range(2):
            gather(0, 3, h * HALF, HALF)
            group_pair(0, 2, h * HALF, HALF)
        gather(1, 0, 0, J)
        quantise_x(0, 0)
        cast_wu(nc.scalar.copy, 0, 0, 2)
        quantise_wu(0, 0)
        cast_wu(nc.scalar.copy, 0, 2, 2)
        for h in range(2):
            gather(1, 1, h * HALF, HALF)
        wd_grouped = [tile("wd_grouped%d" % u, PACK * N // 2, BF16) for u in range(2)]
        interleave(nc.scalar.copy, wd_grouped[0][:], wd_raw[0][:])
        wg_codes = tile_at("wg_codes", [PASSES, 2 * R], U8, 0)
        wu_codes[0, 1] = tile_at("wu_codes01", [R // 2], U32, 2048)[:]
        x_grouped.append(tile_at("x_grouped1", [PACK * J], BF16, 3072))
        quantise_wu(0, 1)
        group_pair(1, 0, 0, HALF)
        nc.scalar.copy(
            wg_codes[:].bitcast(U32).rearrange("p a (t m w) -> p a m t w", t=PACK, w=2),
            wg_raw[:].bitcast(U32).rearrange("p a (m t w) -> p a m t w", t=PACK, w=2),
        )
        group_pair(1, 0, HALF, HALF)
        gather(1, 2, 0, J - CHUNK)
        for s in range(EARLY_UPS):
            up_pass(s, 0, True)
        for s in range(EARLY_GATES):
            gate_pass(s, 0, True)

        for c in range(chunks - 1):
            gather(1, 3, c * CHUNK, CHUNK)
            group_pair(1, 2, c * CHUNK, CHUNK)
        quantise_x(1, 0)
        gate_sums(0)
        gate_sums(1)
        gather(1, 2, J - CHUNK, CHUNK)
        quantise_x(1, 1)
        gate_sums(2)
        gate_sums(3)
        for s in range(4):
            gate(s)
        for s in range(EARLY_UPS, 4):
            up_pass(s, 0, True)
        for t0 in (0, 2):
            cast_wu(nc.vector.tensor_copy, 1, t0, 2)
        for u in range(2):
            quantise_wu(1, u)
        for s in range(4):
            up_sums(s)
        gather(1, 3, J - CHUNK, CHUNK)
        x_codes[1].append(keep.tile([P, CHUNK], U32, name="x_codes1_2", tag="wu_grouped1", align_bytes=64))
        x_codes[1].append(tile("x_codes1_3", CHUNK, U32))
        quantise_x(1, 2)
        gate_sums(4)
        gate_sums(5)
        group_pair(1, 2, J - CHUNK, CHUNK)
        interleave(nc.scalar.copy, wd_grouped[1][:, PACK * P :], wd_raw[1][:, :, P:])
        hidden(0)
        hidden(1)
        wd_codes = tile("wd_codes", N, U32)
        wd_scales = keep.tile([P, N], U8, name="wd_scales", tag="gate0", align_bytes=64)

        def quantise_wd(u):
            cols = slice(u * N // 2, (u + 1) * N // 2)
            quantise(wd_codes[:, cols], wd_scales[:, cols], wd_grouped[u][:])

        quantise_wd(0)
        quantise_h(0, 0, CHUNK)
        quantise_x(1, 3)
        interleave(nc.vector.tensor_copy, wd_grouped[1][:, : PACK * P], wd_raw[1][:, :, :P])
        gate(4)
        gate(5)
        up_sums(4)
        up_sums(5)
        result(0, 0, 4, nc.scalar.copy)
        gate_sums(6)
        gate_sums(7)
        gate(6)
        gate(7)
        hidden(2)
        quantise_wd(1)
        result(0, 1, 5, nc.scalar.copy)
        up_sums(6)
        hidden(3)
        hidden(4)
        quantise_h(1, 0, CHUNK)
        result(1, 0, 4, nc.scalar.copy)
        result(1, 1, 5, nc.scalar.copy)
        up_sums(7)
        hidden(5)
        quantise_h(2, 0, SUB)
        quantise_h(2, SUB, SUB)
        result(2, 0, 6, nc.scalar.copy)
        result(2, 1, 7, nc.scalar.copy)
        hidden(6)
        hidden(7)
        last_banks = (2, 3, 4, 5)
        for j0 in (0, SUB):
            quantise_h(3, j0, SUB)
            for v, slot in enumerate(last_banks):
                nc.tensor.matmul_mx(
                    out=banks[slot][:, j0 : j0 + SUB],
                    lhsT=wd_codes[:, v * P : (v + 1) * P].bitcast(FP8X4),
                    lhsT_scale=wd_scales[:, v * P : (v + 1) * P],
                    rhs=h_codes[3][:, j0 : j0 + SUB].bitcast(FP8X4),
                    rhs_scale=h_scales[3][:, j0 : j0 + SUB],
                    start=True,
                    stop=True,
                )
        for u in range(2):
            y = keep.tile([P, 2, CHUNK], F32, name="y_last%d" % u)
            nc.scalar.copy(y[:, 0, :], banks[last_banks[2 * u]][:, :CHUNK])
            nc.vector.tensor_copy(y[:, 1, :], banks[last_banks[2 * u + 1]][:, :CHUNK])
            nc.sync.dma_start(out_rows[:, 2 * u : 2 * u + 2, J - CHUNK :], y[:])
